import numpy as np
import ml_dtypes


def mxq(x, axis, fmt="e4m3"):
    dtype, down = {"e4m3": (ml_dtypes.float8_e4m3fn, 7), "e5m2": (ml_dtypes.float8_e5m2, 14)}[fmt]
    v = np.moveaxis(np.asarray(x, np.float32).astype(ml_dtypes.bfloat16).astype(np.float64), axis, -1)
    blocks = v.reshape(v.shape[:-1] + (-1, 32))
    amax = np.abs(blocks).max(-1, keepdims=True)
    byte = np.maximum(np.where(amax > 0, np.frexp(amax)[1] - 1 + 127, 0) - down, 1)
    scale = np.exp2(byte - 127.0)
    codes = (blocks / scale).astype(np.float32).astype(dtype).astype(np.float64)
    return np.moveaxis((codes * scale).reshape(v.shape), -1, axis)


WIDE = False


def mx_kscale(k):
    if not WIDE:
        return np.ones(k)
    levels = np.array([10, -10, 5, -5, 0])
    if k % 512:
        return np.exp2(np.random.permutation(np.resize(levels, k // 32))).repeat(32)
    a = np.empty((k // 512, 16))
    for p in range(k // 512):
        a[p, :8] = np.random.permutation(np.resize(levels, 8))
        for g in range(8):
            far = levels[np.abs(levels - a[p, g]) >= 10]
            a[p, g + 8] = far[np.random.randint(len(far))]
    return np.exp2(a.ravel()).repeat(32)


def f64(x):
    return np.asarray(x).astype(np.float64)


def striped(idx):
    return np.tile(idx.reshape(-1, 16).T, (8, 1)).astype(np.uint16)


def unstriped(offs):
    return offs[:16].T.reshape(-1).astype(np.int64)


def pack_weight(w):
    k, n = w.shape
    w = f64(np.asarray(w, np.float32).astype(ml_dtypes.bfloat16)).reshape(k // 32, 32, n)
    amax = np.abs(w).max(1)
    byte = np.clip(np.where(amax > 0, np.frexp(amax)[1] - 1 + 127 - 7, 1), 1, 254)
    scaled = (w * np.exp2(127.0 - byte)[:, None, :]).reshape(k, n).astype(np.float32)
    words = np.ascontiguousarray(scaled.reshape(k // 512, 128, 4, n).transpose(0, 1, 3, 2)).astype(ml_dtypes.float8_e4m3fn).view(np.uint8)
    return words, np.ascontiguousarray(byte.astype(np.uint8).reshape(k // 512, 16, n))


def unpack_weight(words, scales):
    g, p, n, _ = words.shape
    vals = np.ascontiguousarray(words).view(ml_dtypes.float8_e4m3fn).astype(np.float64) * np.repeat(np.exp2(scales.astype(np.float64) - 127.0), 8, axis=1)[..., None]
    return vals.transpose(0, 1, 3, 2).reshape(g * 512, n)


K, T, S, H, N, V = 512, 2048, 512, 512, 256, 256


def setup_inputs():
    n = np.random.standard_normal
    s = mx_kscale(K)[:, None]
    u = mx_kscale(H)
    packed_xT = pack_weight(n((K, T)) * s)
    return {
        "x_words": packed_xT[0],
        "x_scales": packed_xT[1],
        "w1": (n((K, H)) / np.sqrt(K) / s * u).astype(np.float32),
        "w2": (n((H, N)) / np.sqrt(5 * H) / u[:, None]).astype(np.float32),
        "w3": (n((H, N)) / np.sqrt(5 * H) / u[:, None]).astype(np.float32),
        "w4": (n((H, N)) / np.sqrt(5 * H) / u[:, None]).astype(np.float32),
        "w5": (n((H, N)) / np.sqrt(5 * H) / u[:, None]).astype(np.float32),
        "w6": (n((H, N)) / np.sqrt(5 * H) / u[:, None]).astype(np.float32),
        "offs": striped(np.random.permutation(T)[:S]),
        "own": striped(np.random.permutation(S)[:V]),
        "ea": striped(np.random.permutation(S)[:V]),
        "eb": striped(np.random.permutation(S)[:V]),
        "ec": striped(np.random.permutation(S)[:V]),
        "ed": striped(np.random.permutation(S)[:V]),
    }


def reference(x_words, x_scales, w1, w2, w3, w4, w5, w6, offs, own, ea, eb, ec, ed):
    xq = unpack_weight(x_words, x_scales)[:, unstriped(offs)]
    h = mxq(f64(w1), 0, "e4m3").T @ xq
    hown = h[:, unstriped(own)]
    hea = h[:, unstriped(ea)]
    hec = h[:, unstriped(ec)]
    s1 = hea + hec
    d1 = np.abs(hea - hec)
    heb = h[:, unstriped(eb)]
    hed = h[:, unstriped(ed)]
    s2 = heb + hed
    d2 = np.abs(heb - hed)
    return mxq(f64(w2), 0, "e4m3").T @ mxq(hown, 0, "e4m3") + mxq(f64(w3), 0, "e4m3").T @ mxq(s1, 0, "e4m3") + mxq(f64(w4), 0, "e4m3").T @ mxq(d1, 0, "e4m3") + mxq(f64(w5), 0, "e4m3").T @ mxq(s2, 0, "e4m3") + mxq(f64(w6), 0, "e4m3").T @ mxq(d2, 0, "e4m3")

@@ -1,0 +1,171 @@
+from contextlib import ExitStack
+
+import concourse.mybir as mybir
+
+K, T, S, H, N, V = 512, 2048, 512, 512, 256, 256
+FLOPS = 2 * K * H * S + 5 * 2 * H * N * V
+
+F32 = mybir.dt.float32
+BF16 = mybir.dt.bfloat16
+I32 = mybir.dt.int32
+U32 = mybir.dt.uint32
+U16 = mybir.dt.uint16
+U8 = mybir.dt.uint8
+FP8X4 = mybir.dt.float8_e4m3fn_x4
+ALU = mybir.AluOpType
+ACT = mybir.ActivationFunctionType
+
+P = 128
+PACK = 4
+LINE = 4
+W1_SCALAR_M = 24
+
+
+def tile_picked_ymeshcnn_lin_p_kernel(
+    tc, x_words, x_scales, w1, w2, w3, w4, w5, w6, offs, own, ea, eb, ec, ed, out
+):
+    nc = tc.nc
+    with ExitStack() as ctx:
+        keep = ctx.enter_context(tc.tile_pool(name="keep", bufs=1))
+        psum = ctx.enter_context(tc.psum_pool(name="psum", bufs=1))
+
+        def load_list(src, name):
+            tile = keep.tile(list(src.shape), U16, name=name)
+            nc.sync.dma_start(tile[:], src)
+            return tile
+
+        def load_weight(src, name):
+            tile = keep.tile([P, PACK, src.shape[1]], F32, name=name)
+            nc.sync.dma_start(tile[:], src.rearrange("(p j) n -> p j n", j=PACK))
+            return tile
+
+        xs_all = keep.tile([P, T], U8, name="xs_all")
+        nc.vector.memset(xs_all[:].bitcast(I32), 0)
+        offs_t = load_list(offs, "offs_t")
+        xw_all = keep.tile([P, T], U32, name="xw_all")
+        nc.sync.dma_start(xw_all[:].bitcast(I32), x_words[0].rearrange("p n t -> p (n t)").bitcast(I32))
+        for q in range(4):
+            nc.sync.dma_start(xs_all[32 * q : 32 * q + 4, :].bitcast(I32), x_scales[0, 4 * q : 4 * q + 4, :].bitcast(I32))
+        w1_raw = [load_weight(w1[:, u * 256 : (u + 1) * 256], f"w1_raw{u}") for u in range(2)]
+        ea_t = load_list(ea, "ea_t")
+        eb_t = load_list(eb, "eb_t")
+        ec_t = load_list(ec, "ec_t")
+        w4_raw = load_weight(w4, "w4_raw")
+        w3_raw = load_weight(w3, "w3_raw")
+        ed_t = load_list(ed, "ed_t")
+        own_t = load_list(own, "own_t")
+        w6_raw = load_weight(w6, "w6_raw")
+        w5_raw = load_weight(w5, "w5_raw")
+        w2_raw = load_weight(w2, "w2_raw")
+
+        x_codes = keep.tile([P, S], U32, name="x_codes", align_bytes=64)
+        x_scale = keep.tile([P, S], U8, name="x_scale", align_bytes=64)
+        nc.vector.tensor_copy(x_scale[:], xs_all[:].indirect(offs_t[:]))
+        nc.vector.tensor_copy(x_codes[:], xw_all[:].indirect(offs_t[:]))
+
+        w1_bf = keep.tile([P, PACK, P, PACK], BF16, name="w1_bf", align_bytes=64)
+
+        def w1_views(u, m0, m1):
+            dst = w1_bf[:, :, 64 * u + m0 : 64 * u + m1, :].rearrange("p t m j -> p m j t")
+            src = w1_raw[u][:, :, PACK * m0 : PACK * m1].rearrange("p j (m t) -> p m j t", t=PACK)
+            return dst, src
+
+        nc.scalar.activation(*w1_views(0, 0, 64), ACT.Copy)
+        nc.scalar.activation(*w1_views(1, 0, W1_SCALAR_M), ACT.Copy)
+        nc.vector.tensor_copy(*w1_views(1, W1_SCALAR_M, 64))
+
+        def quantize(src, name):
+            width = src.shape[1] // PACK
+            codes = keep.tile([P, width], U32, name=name + "_codes", align_bytes=64)
+            scale = keep.tile([P, width], U8, name=name + "_scale", align_bytes=64)
+            nc.vector.quantize_mx(out=codes[:].bitcast(FP8X4), scales=scale[:], in_=src)
+            return codes, scale
+
+        def mx(acc, lhs, lcols, rhs, rcols, start, stop):
+            nc.tensor.matmul_mx(
+                out=acc, lhsT=lhs[0][:, lcols].bitcast(FP8X4), lhsT_scale=lhs[1][:, lcols],
+                rhs=rhs[0][:, rcols].bitcast(FP8X4), rhs_scale=rhs[1][:, rcols], start=start, stop=stop)
+
+        h = []
+        for t in range(PACK):
+            w1_q = quantize(w1_bf[:, t, :, :].rearrange("p m j -> p (m j)"), f"w1_{t}")
+            h_t = keep.tile([P, S], F32, name=f"h{t}")
+            if t == 0:
+                for u in range(2):
+                    cols = slice(256 * u, 256 * (u + 1))
+                    acc = psum.tile([P, 256], F32, name=f"h0_acc{u}")
+                    mx(acc[:], w1_q, slice(0, P), (x_codes, x_scale), cols, True, True)
+                    if u == 0:
+                        nc.scalar.activation(h_t[:, cols], acc[:], ACT.Copy)
+                    else:
+                        nc.vector.tensor_copy(h_t[:, cols], acc[:])
+            else:
+                acc = psum.tile([P, S], F32, name=f"h_acc{t}")
+                mx(acc[:], w1_q, slice(0, P), (x_codes, x_scale), slice(0, S), True, True)
+                nc.scalar.activation(h_t[:], acc[:], ACT.Copy)
+            h.append(h_t)
+
+        def interleave(src, name, func):
+            width = src.shape[2]
+            dst = keep.tile([P, width, PACK], BF16, name=name, align_bytes=64)
+            nc.scalar.activation(
+                dst[:].rearrange("p (c i) t -> p c t i", i=LINE),
+                src[:].rearrange("p t (c i) -> p c t i", i=LINE), func)
+            return dst[:].rearrange("p v t -> p (v t)")
+
+        out_acc = [psum.tile([P, V], F32, name=f"out_acc{m}") for m in range(2)]
+
+        def product(w_q, v_q, start, stop):
+            for m in range(2):
+                mx(out_acc[m][:], w_q, slice(P * m, P * (m + 1)), v_q, slice(0, V), start, stop)
+
+        def flat(tile):
+            return tile[:].rearrange("p t v -> p (t v)")
+
+        w4_bf = interleave(w4_raw, "w4_bf", ACT.Copy)
+        w3_bf = interleave(w3_raw, "w3_bf", ACT.Copy)
+        w6_bf = interleave(w6_raw, "w6_bf", ACT.Copy)
+        w5_bf = interleave(w5_raw, "w5_bf", ACT.Copy)
+
+        ha = keep.tile([P, PACK, V], F32, name="ha")
+        hb = keep.tile([P, PACK, V], F32, name="hb")
+        diff1 = keep.tile([P, PACK, V], F32, name="diff", tag="diff")
+        for t in range(PACK):
+            nc.vector.tensor_copy(ha[:, t, :], h[t][:].indirect(ea_t[:]))
+            nc.vector.tensor_copy(hb[:, t, :], h[t][:].indirect(eb_t[:]))
+            nc.vector.tensor_tensor(diff1[:, t, :], h[t][:].indirect(ec_t[:]), ha[:, t, :], ALU.subtract)
+        d1_bf = interleave(diff1, "d1_bf", ACT.Abs)
+        sum1 = keep.tile([P, PACK, V], F32, name="sum1")
+        nc.vector.scalar_tensor_tensor(flat(sum1), flat(ha), 2.0, flat(diff1), ALU.mult, ALU.add)
+        s1_bf = interleave(sum1, "s1_bf", ACT.Copy)
+        w2_bf = interleave(w2_raw, "w2_bf", ACT.Copy)
+
+        diff2 = keep.tile([P, PACK, V], F32, name="ha", tag="ha")
+        for t in range(PACK):
+            nc.vector.tensor_tensor(diff2[:, t, :], h[t][:].indirect(ed_t[:]), hb[:, t, :], ALU.subtract)
+        d2_bf = interleave(diff2, "d2_bf", ACT.Abs)
+        w4_q = quantize(w4_bf, "w4")
+        sum2 = keep.tile([P, PACK, V], F32, name="sum2")
+        nc.vector.scalar_tensor_tensor(flat(sum2), flat(hb), 2.0, flat(diff2), ALU.mult, ALU.add)
+        s2_bf = interleave(sum2, "s2_bf", ACT.Copy)
+        product(w4_q, quantize(d1_bf, "d1"), True, False)
+        product(quantize(w3_bf, "w3"), quantize(s1_bf, "s1"), False, False)
+        w6_q = quantize(w6_bf, "w6")
+        w5_q = quantize(w5_bf, "w5")
+        w2_q = quantize(w2_bf, "w2")
+
+        hown = keep.tile([P, PACK, V], F32, name="hb", tag="hb")
+        for t in range(PACK):
+            nc.vector.tensor_copy(hown[:, t, :], h[t][:].indirect(own_t[:]))
+        own_bf = interleave(hown, "own_bf", ACT.Copy)
+        product(w6_q, quantize(d2_bf, "d2"), False, False)
+        product(w5_q, quantize(s2_bf, "s2"), False, False)
+        product(w2_q, quantize(own_bf, "own"), False, True)
+
+        for m in range(2):
+            res = keep.tile([P, V], F32, name=f"res{m}")
+            if m == 0:
+                nc.scalar.activation(res[:], out_acc[m][:], ACT.Copy)
+            else:
+                nc.vector.tensor_copy(res[:], out_acc[m][:])
+            nc.sync.dma_start(out[P * m : P * (m + 1), :], res[:])

@@ -1,6 +1,7 @@
 from contextlib import ExitStack
 
 import concourse.mybir as mybir
+from concourse.masks import make_identity
 
 K, T, S, H, N, V = 512, 2048, 512, 512, 256, 256
 FLOPS = 2 * K * H * S + 5 * 2 * H * N * V
@@ -35,7 +36,7 @@ def tile_picked_ymeshcnn_lin_p_kernel(
             return tile
 
         def load_weight(src, name):
-            tile = keep.tile([P, PACK, src.shape[1]], F32, name=name)
+            tile = keep.tile([P, PACK, src.shape[1]], F32, name=name, align_bytes=64)
             nc.sync.dma_start(tile[:], src.rearrange("(p j) n -> p j n", j=PACK))
             return tile
 
@@ -74,9 +75,9 @@ def tile_picked_ymeshcnn_lin_p_kernel(
         nc.scalar.activation(*w1_views(1, 0, W1_SCALAR_M), ACT.Copy)
         nc.vector.tensor_copy(*w1_views(1, W1_SCALAR_M, 64))
 
-        def quantize(src, name):
+        def quantize(src, name, slot=None):
             width = src.shape[1] // PACK
-            codes = keep.tile([P, width], U32, name=name + "_codes", align_bytes=64)
+            codes = keep.tile([P, width], U32, name=name + "_codes", tag=slot or name + "_codes", align_bytes=64)
             scale = keep.tile([P, width], U8, name=name + "_scale", align_bytes=64)
             nc.vector.quantize_mx(out=codes[:].bitcast(FP8X4), scales=scale[:], in_=src)
             return codes, scale
@@ -86,86 +87,118 @@ def tile_picked_ymeshcnn_lin_p_kernel(
                 out=acc, lhsT=lhs[0][:, lcols].bitcast(FP8X4), lhsT_scale=lhs[1][:, lcols],
                 rhs=rhs[0][:, rcols].bitcast(FP8X4), rhs_scale=rhs[1][:, rcols], start=start, stop=stop)
 
+        banks = [psum.tile([P, 512], F32, name=f"bank{b}") for b in range(6)]
+        ident = keep.tile([P, P], F32, name="ident")
+        make_identity(nc, ident[:])
         h = []
         for t in range(PACK):
             w1_q = quantize(w1_bf[:, t, :, :].rearrange("p m j -> p (m j)"), f"w1_{t}")
-            h_t = keep.tile([P, S], F32, name=f"h{t}")
+            h_t = keep.tile([P, S], F32, name=f"h{t}", align_bytes=64)
             if t == 0:
                 for u in range(2):
                     cols = slice(256 * u, 256 * (u + 1))
-                    acc = psum.tile([P, 256], F32, name=f"h0_acc{u}")
-                    mx(acc[:], w1_q, slice(0, P), (x_codes, x_scale), cols, True, True)
-                    if u == 0:
-                        nc.scalar.activation(h_t[:, cols], acc[:], ACT.Copy)
-                    else:
-                        nc.vector.tensor_copy(h_t[:, cols], acc[:])
+                    acc = banks[u][:, 0:256]
+                    mx(acc, w1_q, slice(0, P), (x_codes, x_scale), cols, True, True)
+                    nc.vector.tensor_copy(h_t[:, cols], acc)
             else:
-                acc = psum.tile([P, S], F32, name=f"h_acc{t}")
-                mx(acc[:], w1_q, slice(0, P), (x_codes, x_scale), slice(0, S), True, True)
-                nc.scalar.activation(h_t[:], acc[:], ACT.Copy)
+                acc = banks[1 + t][:]
+                mx(acc, w1_q, slice(0, P), (x_codes, x_scale), slice(0, S), True, True)
+                nc.scalar.activation(h_t[:], acc, ACT.Copy)
             h.append(h_t)
 
-        def interleave(src, name, func):
-            width = src.shape[2]
-            dst = keep.tile([P, width, PACK], BF16, name=name, align_bytes=64)
+        def interleave(src, dst, func):
             nc.scalar.activation(
-                dst[:].rearrange("p (c i) t -> p c t i", i=LINE),
+                dst.rearrange("p (c i t) -> p c t i", i=LINE, t=PACK),
                 src[:].rearrange("p t (c i) -> p c t i", i=LINE), func)
-            return dst[:].rearrange("p v t -> p (v t)")
 
-        out_acc = [psum.tile([P, V], F32, name=f"out_acc{m}") for m in range(2)]
+        def bf_tile(name, width, slot=None):
+            return keep.tile([P, width], BF16, name=name, tag=slot or name, align_bytes=64)
 
-        def product(w_q, v_q, start, stop):
+        def f32_tile(name, slot=None):
+            return keep.tile([P, PACK, V], F32, name=name, tag=slot or name, align_bytes=64)
+
+        out_acc = [banks[5][:, 0:V], banks[2][:, 0:V]]
+
+        def product(w_q, w0, v_q, v0, start, stop):
             for m in range(2):
-                mx(out_acc[m][:], w_q, slice(P * m, P * (m + 1)), v_q, slice(0, V), start, stop)
+                mx(out_acc[m], w_q, slice(w0 + P * m, w0 + P * (m + 1)), v_q, slice(v0, v0 + V), start, stop)
 
-        def flat(tile):
-            return tile[:].rearrange("p t v -> p (t v)")
+        def add_transposed(src, t, acc, times, first, last):
+            steps = [(vb, k) for vb in range(2) for k in range(times)]
+            for n, (vb, k) in enumerate(steps):
+                at = P * (2 * vb + t % 2)
+                nc.tensor.matmul(acc[t // 2][:, at : at + P], src[:, t, P * vb : P * (vb + 1)], ident[:],
+                                 start=(first and t % 2 == 0 and n == 0),
+                                 stop=(last and t % 2 == 1 and n == len(steps) - 1), is_transpose=True)
 
-        w4_bf = interleave(w4_raw, "w4_bf", ACT.Copy)
-        w3_bf = interleave(w3_raw, "w3_bf", ACT.Copy)
-        w6_bf = interleave(w6_raw, "w6_bf", ACT.Copy)
-        w5_bf = interleave(w5_raw, "w5_bf", ACT.Copy)
+        def turn_back(acc, rows, back):
+            for u in range(2):
+                half = rows[:, 512 * u : 512 * (u + 1)]
+                nc.scalar.activation(half.rearrange("v (b p e) -> v b p e", b=2, e=2),
+                                     acc[u][:].rearrange("v (b e p) -> v b p e", b=2, e=2), ACT.Copy)
+                words = half.bitcast(F32)
+                for vb in range(2):
+                    nc.tensor.transpose(back[:, P * (2 * vb + u) : P * (2 * vb + u + 1)], words[:, P * vb : P * (vb + 1)], ident[:])
 
-        ha = keep.tile([P, PACK, V], F32, name="ha")
-        hb = keep.tile([P, PACK, V], F32, name="hb")
-        diff1 = keep.tile([P, PACK, V], F32, name="diff", tag="diff")
+        def copy_back(back, name):
+            dst = bf_tile(name, V * PACK)
+            nc.scalar.copy(dst[:].bitcast(F32).rearrange("p (b v u) -> p b v u", b=2, u=2),
+                           back[:].rearrange("p (b u v) -> p b v u", b=2, u=2))
+            return dst
+
+        W = N * PACK
+        w43_bf = bf_tile("w43_bf", 2 * W)
+        w65_bf = bf_tile("w65_bf", 2 * W)
+        w2_bf = bf_tile("w2_bf", W)
+        interleave(w4_raw, w43_bf[:, 0:W], ACT.Copy)
+        interleave(w3_raw, w43_bf[:, W : 2 * W], ACT.Copy)
+        interleave(w6_raw, w65_bf[:, 0:W], ACT.Copy)
+        interleave(w5_raw, w65_bf[:, W : 2 * W], ACT.Copy)
+        interleave(w2_raw, w2_bf[:], ACT.Copy)
+
+        ha = f32_tile("ha")
+        hb = f32_tile("hb")
+        diff1 = f32_tile("diff1")
+        diff2 = f32_tile("diff2")
+        acc1, acc2 = banks[0:2], [banks[5], banks[2]]
         for t in range(PACK):
             nc.vector.tensor_copy(ha[:, t, :], h[t][:].indirect(ea_t[:]))
+            add_transposed(ha, t, acc1, 2, True, False)
             nc.vector.tensor_copy(hb[:, t, :], h[t][:].indirect(eb_t[:]))
             nc.vector.tensor_tensor(diff1[:, t, :], h[t][:].indirect(ec_t[:]), ha[:, t, :], ALU.subtract)
-        d1_bf = interleave(diff1, "d1_bf", ACT.Abs)
-        sum1 = keep.tile([P, PACK, V], F32, name="sum1")
-        nc.vector.scalar_tensor_tensor(flat(sum1), flat(ha), 2.0, flat(diff1), ALU.mult, ALU.add)
-        s1_bf = interleave(sum1, "s1_bf", ACT.Copy)
-        w2_bf = interleave(w2_raw, "w2_bf", ACT.Copy)
-
-        diff2 = keep.tile([P, PACK, V], F32, name="ha", tag="ha")
+            add_transposed(diff1, t, acc1, 1, False, True)
+            add_transposed(hb, t, acc2, 2, True, False)
+        d_bf = bf_tile("d_bf", 2 * W, "w2_raw")
+        rows = bf_tile("rows", 2 * W, "diff1")
+        interleave(diff1, d_bf[:, 0:W], ACT.Abs)
+        turn_back(acc1, rows[:, 0:W], banks[3])
         for t in range(PACK):
             nc.vector.tensor_tensor(diff2[:, t, :], h[t][:].indirect(ed_t[:]), hb[:, t, :], ALU.subtract)
-        d2_bf = interleave(diff2, "d2_bf", ACT.Abs)
-        w4_q = quantize(w4_bf, "w4")
-        sum2 = keep.tile([P, PACK, V], F32, name="sum2")
-        nc.vector.scalar_tensor_tensor(flat(sum2), flat(hb), 2.0, flat(diff2), ALU.mult, ALU.add)
-        s2_bf = interleave(sum2, "s2_bf", ACT.Copy)
-        product(w4_q, quantize(d1_bf, "d1"), True, False)
-        product(quantize(w3_bf, "w3"), quantize(s1_bf, "s1"), False, False)
-        w6_q = quantize(w6_bf, "w6")
-        w5_q = quantize(w5_bf, "w5")
-        w2_q = quantize(w2_bf, "w2")
+            add_transposed(diff2, t, acc2, 1, False, True)
+        interleave(diff2, d_bf[:, W : 2 * W], ACT.Abs)
+        turn_back(acc2, rows[:, W : 2 * W], banks[4])
+        s1_bf = copy_back(banks[3], "s1_bf")
+        s2_bf = copy_back(banks[4], "s2_bf")
 
-        hown = keep.tile([P, PACK, V], F32, name="hb", tag="hb")
+        w43_q = quantize(w43_bf[:], "w43")
+        w65_q = quantize(w65_bf[:], "w65")
+        d_q = quantize(d_bf[:], "d")
+        product(w43_q, 0, d_q, 0, True, False)
+        product(w65_q, 0, d_q, V, False, False)
+        hown = f32_tile("hown", "w2_raw")
         for t in range(PACK):
             nc.vector.tensor_copy(hown[:, t, :], h[t][:].indirect(own_t[:]))
-        own_bf = interleave(hown, "own_bf", ACT.Copy)
-        product(w6_q, quantize(d2_bf, "d2"), False, False)
-        product(w5_q, quantize(s2_bf, "s2"), False, False)
-        product(w2_q, quantize(own_bf, "own"), False, True)
+        own_bf = bf_tile("own_bf", W, "diff2")
+        interleave(hown, own_bf[:], ACT.Copy)
+        product(w43_q, N, quantize(s1_bf[:], "s1"), 0, False, False)
+        w2_q = quantize(w2_bf[:], "w2", "h0")
+        product(w65_q, N, quantize(s2_bf[:], "s2"), 0, False, False)
+        product(w2_q, 0, quantize(own_bf[:], "own"), 0, False, True)
 
         for m in range(2):
             res = keep.tile([P, V], F32, name=f"res{m}")
             if m == 0:
-                nc.scalar.activation(res[:], out_acc[m][:], ACT.Copy)
+                nc.scalar.activation(res[:], out_acc[m], ACT.Copy)
             else:
-                nc.vector.tensor_copy(res[:], out_acc[m][:])
+                nc.vector.tensor_copy(res[:], out_acc[m])
             nc.sync.dma_start(out[P * m : P * (m + 1), :], res[:])

@@ -87,7 +87,7 @@ def tile_picked_ymeshcnn_lin_p_kernel(
                 out=acc, lhsT=lhs[0][:, lcols].bitcast(FP8X4), lhsT_scale=lhs[1][:, lcols],
                 rhs=rhs[0][:, rcols].bitcast(FP8X4), rhs_scale=rhs[1][:, rcols], start=start, stop=stop)
 
-        banks = [psum.tile([P, 512], F32, name=f"bank{b}") for b in range(6)]
+        banks = [psum.tile([P, 512], F32, name=f"bank{b}") for b in range(8)]
         ident = keep.tile([P, P], F32, name="ident")
         make_identity(nc, ident[:])
         h = []
@@ -109,7 +109,7 @@ def tile_picked_ymeshcnn_lin_p_kernel(
         def interleave(src, dst, func):
             nc.scalar.activation(
                 dst.rearrange("p (c i t) -> p c t i", i=LINE, t=PACK),
-                src[:].rearrange("p t (c i) -> p c t i", i=LINE), func)
+                src.rearrange("p t (c i) -> p c t i", i=LINE), func)
 
         def bf_tile(name, width, slot=None):
             return keep.tile([P, width], BF16, name=name, tag=slot or name, align_bytes=64)
@@ -117,11 +117,15 @@ def tile_picked_ymeshcnn_lin_p_kernel(
         def f32_tile(name, slot=None):
             return keep.tile([P, PACK, V], F32, name=name, tag=slot or name, align_bytes=64)
 
-        out_acc = [banks[5][:, 0:V], banks[2][:, 0:V]]
+        out_acc = [[banks[5][:, 0:P], banks[2][:, 0:P]], [banks[6][:, 0:P], banks[7][:, 0:P]]]
 
-        def product(w_q, w0, v_q, v0, start, stop):
+        def half_product(w_q, w0, v_q, v0, vb, start, stop):
             for m in range(2):
-                mx(out_acc[m], w_q, slice(w0 + P * m, w0 + P * (m + 1)), v_q, slice(v0, v0 + V), start, stop)
+                mx(out_acc[vb][m], w_q, slice(w0 + P * m, w0 + P * (m + 1)), v_q, slice(v0, v0 + P), start, stop)
+
+        def product(w_q, w0, v_q, v0, start):
+            for vb in range(2):
+                half_product(w_q, w0, v_q, v0 + P * vb, vb, start, False)
 
         def add_transposed(src, t, acc, times, first, last):
             steps = [(vb, k) for vb in range(2) for k in range(times)]
@@ -150,11 +154,11 @@ def tile_picked_ymeshcnn_lin_p_kernel(
         w43_bf = bf_tile("w43_bf", 2 * W)
         w65_bf = bf_tile("w65_bf", 2 * W)
         w2_bf = bf_tile("w2_bf", W)
-        interleave(w4_raw, w43_bf[:, 0:W], ACT.Copy)
-        interleave(w3_raw, w43_bf[:, W : 2 * W], ACT.Copy)
-        interleave(w6_raw, w65_bf[:, 0:W], ACT.Copy)
-        interleave(w5_raw, w65_bf[:, W : 2 * W], ACT.Copy)
-        interleave(w2_raw, w2_bf[:], ACT.Copy)
+        interleave(w4_raw[:], w43_bf[:, 0:W], ACT.Copy)
+        interleave(w3_raw[:], w43_bf[:, W : 2 * W], ACT.Copy)
+        interleave(w6_raw[:], w65_bf[:, 0:W], ACT.Copy)
+        interleave(w5_raw[:], w65_bf[:, W : 2 * W], ACT.Copy)
+        interleave(w2_raw[:], w2_bf[:], ACT.Copy)
 
         ha = f32_tile("ha")
         hb = f32_tile("hb")
@@ -170,35 +174,38 @@ def tile_picked_ymeshcnn_lin_p_kernel(
             add_transposed(hb, t, acc2, 2, True, False)
         d_bf = bf_tile("d_bf", 2 * W, "w2_raw")
         rows = bf_tile("rows", 2 * W, "diff1")
-        interleave(diff1, d_bf[:, 0:W], ACT.Abs)
+        interleave(diff1[:], d_bf[:, 0:W], ACT.Abs)
         turn_back(acc1, rows[:, 0:W], banks[3])
         for t in range(PACK):
             nc.vector.tensor_tensor(diff2[:, t, :], h[t][:].indirect(ed_t[:]), hb[:, t, :], ALU.subtract)
             add_transposed(diff2, t, acc2, 1, False, True)
-        interleave(diff2, d_bf[:, W : 2 * W], ACT.Abs)
+        interleave(diff2[:], d_bf[:, W : 2 * W], ACT.Abs)
         turn_back(acc2, rows[:, W : 2 * W], banks[4])
         s1_bf = copy_back(banks[3], "s1_bf")
         s2_bf = copy_back(banks[4], "s2_bf")
 
         w43_q = quantize(w43_bf[:], "w43")
         w65_q = quantize(w65_bf[:], "w65")
+        w2_q = quantize(w2_bf[:], "w2")
         d_q = quantize(d_bf[:], "d")
-        product(w43_q, 0, d_q, 0, True, False)
-        product(w65_q, 0, d_q, V, False, False)
-        hown = f32_tile("hown", "w2_raw")
-        for t in range(PACK):
-            nc.vector.tensor_copy(hown[:, t, :], h[t][:].indirect(own_t[:]))
-        own_bf = bf_tile("own_bf", W, "diff2")
-        interleave(hown, own_bf[:], ACT.Copy)
-        product(w43_q, N, quantize(s1_bf[:], "s1"), 0, False, False)
-        w2_q = quantize(w2_bf[:], "w2", "h0")
-        product(w65_q, N, quantize(s2_bf[:], "s2"), 0, False, False)
-        product(w2_q, 0, quantize(own_bf[:], "own"), 0, False, True)
-
-        for m in range(2):
-            res = keep.tile([P, V], F32, name=f"res{m}")
-            if m == 0:
-                nc.scalar.activation(res[:], out_acc[m], ACT.Copy)
+        product(w43_q, 0, d_q, 0, True)
+        product(w65_q, 0, d_q, V, False)
+        hown = keep.tile([P, 2 * PACK * P], F32, name="hown", tag="diff2", align_bytes=64)
+        own_bf = []
+        for vb in range(2):
+            half = hown[:, PACK * P * vb : PACK * P * (vb + 1)].rearrange("p (t v) -> p t v", t=PACK)
+            for t in range(PACK):
+                nc.vector.tensor_copy(half[:, t, :], h[t][:].indirect(own_t[:, 8 * vb : 8 * (vb + 1)]))
+            own_bf.append(bf_tile(f"own_bf{vb}", PACK * P))
+            interleave(half, own_bf[vb][:], ACT.Copy)
+        product(w43_q, N, quantize(s1_bf[:], "s1"), 0, False)
+        product(w65_q, N, quantize(s2_bf[:], "s2"), 0, False)
+        for vb in range(2):
+            half_product(w2_q, 0, quantize(own_bf[vb][:], f"own{vb}"), 0, vb, False, True)
+            res = keep.tile([P, 2, P], F32, name=f"res{vb}")
+            nc.scalar.activation(res[:, 0, :], out_acc[vb][0], ACT.Copy)
+            if vb == 0:
+                nc.scalar.activation(res[:, 1, :], out_acc[vb][1], ACT.Copy)
             else:
-                nc.vector.tensor_copy(res[:], out_acc[m])
-            nc.sync.dma_start(out[P * m : P * (m + 1), :], res[:])
+                nc.vector.tensor_copy(res[:, 1, :], out_acc[vb][1])
+            nc.sync.dma_start(out[:, P * vb : P * (vb + 1)].rearrange("(m p) v -> p m v", m=2), res[:])

@@ -117,7 +117,7 @@ def tile_picked_ymeshcnn_lin_p_kernel(
         def f32_tile(name, slot=None):
             return keep.tile([P, PACK, V], F32, name=name, tag=slot or name, align_bytes=64)
 
-        out_acc = [[banks[5][:, 0:P], banks[2][:, 0:P]], [banks[6][:, 0:P], banks[7][:, 0:P]]]
+        out_acc = [[banks[0][:, 0:P], banks[1][:, 0:P]], [banks[6][:, 0:P], banks[7][:, 0:P]]]
 
         def half_product(w_q, w0, v_q, v0, vb, start, stop):
             for m in range(2):
@@ -135,14 +135,13 @@ def tile_picked_ymeshcnn_lin_p_kernel(
                                  start=(first and t % 2 == 0 and n == 0),
                                  stop=(last and t % 2 == 1 and n == len(steps) - 1), is_transpose=True)
 
-        def turn_back(acc, rows, back):
-            for u in range(2):
-                half = rows[:, 512 * u : 512 * (u + 1)]
-                nc.scalar.activation(half.rearrange("v (b p e) -> v b p e", b=2, e=2),
-                                     acc[u][:].rearrange("v (b e p) -> v b p e", b=2, e=2), ACT.Copy)
-                words = half.bitcast(F32)
-                for vb in range(2):
-                    nc.tensor.transpose(back[:, P * (2 * vb + u) : P * (2 * vb + u + 1)], words[:, P * vb : P * (vb + 1)], ident[:])
+        def turn_back(acc, rows, back, u):
+            half = rows[:, 512 * u : 512 * (u + 1)]
+            nc.scalar.activation(half.rearrange("v (b p e) -> v b p e", b=2, e=2),
+                                 acc[u][:].rearrange("v (b e p) -> v b p e", b=2, e=2), ACT.Copy)
+            words = half.bitcast(F32)
+            for vb in range(2):
+                nc.tensor.transpose(back[:, P * (2 * vb + u) : P * (2 * vb + u + 1)], words[:, P * vb : P * (vb + 1)], ident[:])
 
         def copy_back(back, name):
             dst = bf_tile(name, V * PACK)
@@ -172,24 +171,27 @@ def tile_picked_ymeshcnn_lin_p_kernel(
             nc.vector.tensor_tensor(diff1[:, t, :], h[t][:].indirect(ec_t[:]), ha[:, t, :], ALU.subtract)
             add_transposed(diff1, t, acc1, 1, False, True)
             add_transposed(hb, t, acc2, 2, True, False)
-        d_bf = bf_tile("d_bf", 2 * W, "w2_raw")
-        rows = bf_tile("rows", 2 * W, "diff1")
+        stage = bf_tile("stage", 4 * W, "w2_raw")
+        d_bf, rows1, rows2 = stage[:, 0 : 2 * W], stage[:, 2 * W : 3 * W], stage[:, 3 * W : 4 * W]
+        turn_back(acc1, rows1, banks[3], 0)
         interleave(diff1[:], d_bf[:, 0:W], ACT.Abs)
-        turn_back(acc1, rows[:, 0:W], banks[3])
+        turn_back(acc1, rows1, banks[3], 1)
         for t in range(PACK):
             nc.vector.tensor_tensor(diff2[:, t, :], h[t][:].indirect(ed_t[:]), hb[:, t, :], ALU.subtract)
             add_transposed(diff2, t, acc2, 1, False, True)
+        turn_back(acc2, rows2, banks[4], 0)
         interleave(diff2[:], d_bf[:, W : 2 * W], ACT.Abs)
-        turn_back(acc2, rows[:, W : 2 * W], banks[4])
+        turn_back(acc2, rows2, banks[4], 1)
         s1_bf = copy_back(banks[3], "s1_bf")
         s2_bf = copy_back(banks[4], "s2_bf")
 
         w43_q = quantize(w43_bf[:], "w43")
         w65_q = quantize(w65_bf[:], "w65")
-        w2_q = quantize(w2_bf[:], "w2")
-        d_q = quantize(d_bf[:], "d")
+        d_q = quantize(d_bf, "d")
         product(w43_q, 0, d_q, 0, True)
         product(w65_q, 0, d_q, V, False)
+        product(w43_q, N, quantize(s1_bf[:], "s1"), 0, False)
+        product(w65_q, N, quantize(s2_bf[:], "s2"), 0, False)
         hown = keep.tile([P, 2 * PACK * P], F32, name="hown", tag="diff2", align_bytes=64)
         own_bf = []
         for vb in range(2):
@@ -197,9 +199,13 @@ def tile_picked_ymeshcnn_lin_p_kernel(
             for t in range(PACK):
                 nc.vector.tensor_copy(half[:, t, :], h[t][:].indirect(own_t[:, 8 * vb : 8 * (vb + 1)]))
             own_bf.append(bf_tile(f"own_bf{vb}", PACK * P))
-            interleave(half, own_bf[vb][:], ACT.Copy)
-        product(w43_q, N, quantize(s1_bf[:], "s1"), 0, False)
-        product(w65_q, N, quantize(s2_bf[:], "s2"), 0, False)
+            if vb == 0:
+                interleave(half, own_bf[vb][:], ACT.Copy)
+            else:
+                interleave(half[:, :, 0:64], own_bf[vb][:, 0:256], ACT.Copy)
+                nc.vector.tensor_copy(own_bf[vb][:, 256:512].rearrange("p (c i t) -> p c t i", i=LINE, t=PACK),
+                                      half[:, :, 64:128].rearrange("p t (c i) -> p c t i", i=LINE))
+        w2_q = quantize(w2_bf[:], "w2", "h0")
         for vb in range(2):
             half_product(w2_q, 0, quantize(own_bf[vb][:], f"own{vb}"), 0, vb, False, True)
             res = keep.tile([P, 2, P], F32, name=f"res{vb}")

@@ -1,7 +1,6 @@
 from contextlib import ExitStack
 
 import concourse.mybir as mybir
-from concourse.masks import make_identity
 
 K, T, S, H, N, V = 512, 2048, 512, 512, 256, 256
 FLOPS = 2 * K * H * S + 5 * 2 * H * N * V
@@ -20,6 +19,7 @@ P = 128
 PACK = 4
 LINE = 4
 W1_SCALAR_M = 24
+VECTOR_GATHERS = 3
 
 
 def tile_picked_ymeshcnn_lin_p_kernel(
@@ -49,10 +49,10 @@ def tile_picked_ymeshcnn_lin_p_kernel(
             nc.sync.dma_start(xs_all[32 * q : 32 * q + 4, :].bitcast(I32), x_scales[0, 4 * q : 4 * q + 4, :].bitcast(I32))
         w1_raw = [load_weight(w1[:, u * 256 : (u + 1) * 256], f"w1_raw{u}") for u in range(2)]
         ea_t = load_list(ea, "ea_t")
-        eb_t = load_list(eb, "eb_t")
         ec_t = load_list(ec, "ec_t")
         w4_raw = load_weight(w4, "w4_raw")
         w3_raw = load_weight(w3, "w3_raw")
+        eb_t = load_list(eb, "eb_t")
         ed_t = load_list(ed, "ed_t")
         own_t = load_list(own, "own_t")
         w6_raw = load_weight(w6, "w6_raw")
@@ -75,9 +75,9 @@ def tile_picked_ymeshcnn_lin_p_kernel(
         nc.scalar.activation(*w1_views(1, 0, W1_SCALAR_M), ACT.Copy)
         nc.vector.tensor_copy(*w1_views(1, W1_SCALAR_M, 64))
 
-        def quantize(src, name, slot=None):
+        def quantize(src, name):
             width = src.shape[1] // PACK
-            codes = keep.tile([P, width], U32, name=name + "_codes", tag=slot or name + "_codes", align_bytes=64)
+            codes = keep.tile([P, width], U32, name=name + "_codes", align_bytes=64)
             scale = keep.tile([P, width], U8, name=name + "_scale", align_bytes=64)
             nc.vector.quantize_mx(out=codes[:].bitcast(FP8X4), scales=scale[:], in_=src)
             return codes, scale
@@ -87,9 +87,7 @@ def tile_picked_ymeshcnn_lin_p_kernel(
                 out=acc, lhsT=lhs[0][:, lcols].bitcast(FP8X4), lhsT_scale=lhs[1][:, lcols],
                 rhs=rhs[0][:, rcols].bitcast(FP8X4), rhs_scale=rhs[1][:, rcols], start=start, stop=stop)
 
-        banks = [psum.tile([P, 512], F32, name=f"bank{b}") for b in range(8)]
-        ident = keep.tile([P, P], F32, name="ident")
-        make_identity(nc, ident[:])
+        banks = [psum.tile([P, 512], F32, name=f"bank{b}") for b in range(7)]
         h = []
         for t in range(PACK):
             w1_q = quantize(w1_bf[:, t, :, :].rearrange("p m j -> p (m j)"), f"w1_{t}")
@@ -106,10 +104,11 @@ def tile_picked_ymeshcnn_lin_p_kernel(
                 nc.scalar.activation(h_t[:], acc, ACT.Copy)
             h.append(h_t)
 
-        def interleave(src, dst, func):
-            nc.scalar.activation(
-                dst.rearrange("p (c i t) -> p c t i", i=LINE, t=PACK),
-                src.rearrange("p t (c i) -> p c t i", i=LINE), func)
+        def woven(dst):
+            return dst.rearrange("p (c i t) -> p c t i", i=LINE, t=PACK)
+
+        def planes(src):
+            return src.rearrange("p t (c i) -> p c t i", i=LINE)
 
         def bf_tile(name, width, slot=None):
             return keep.tile([P, width], BF16, name=name, tag=slot or name, align_bytes=64)
@@ -117,101 +116,65 @@ def tile_picked_ymeshcnn_lin_p_kernel(
         def f32_tile(name, slot=None):
             return keep.tile([P, PACK, V], F32, name=name, tag=slot or name, align_bytes=64)
 
-        out_acc = [[banks[0][:, 0:P], banks[1][:, 0:P]], [banks[6][:, 0:P], banks[7][:, 0:P]]]
+        def gather(dst, t, places, on_vector):
+            if on_vector:
+                nc.vector.tensor_copy(dst, h[t][:].indirect(places))
+            else:
+                nc.scalar.activation(dst, h[t][:].indirect(places), ACT.Copy)
 
-        def half_product(w_q, w0, v_q, v0, vb, start, stop):
+        out_acc = [banks[5][:, 0:V], banks[6][:, 0:V]]
+
+        def product(w_q, w0, v_q, start, stop):
             for m in range(2):
-                mx(out_acc[vb][m], w_q, slice(w0 + P * m, w0 + P * (m + 1)), v_q, slice(v0, v0 + P), start, stop)
-
-        def product(w_q, w0, v_q, v0, start):
-            for vb in range(2):
-                half_product(w_q, w0, v_q, v0 + P * vb, vb, start, False)
-
-        def add_transposed(src, t, acc, times, first, last):
-            steps = [(vb, k) for vb in range(2) for k in range(times)]
-            for n, (vb, k) in enumerate(steps):
-                at = P * (2 * vb + t % 2)
-                nc.tensor.matmul(acc[t // 2][:, at : at + P], src[:, t, P * vb : P * (vb + 1)], ident[:],
-                                 start=(first and t % 2 == 0 and n == 0),
-                                 stop=(last and t % 2 == 1 and n == len(steps) - 1), is_transpose=True)
-
-        def turn_back(acc, rows, back, u):
-            half = rows[:, 512 * u : 512 * (u + 1)]
-            nc.scalar.activation(half.rearrange("v (b p e) -> v b p e", b=2, e=2),
-                                 acc[u][:].rearrange("v (b e p) -> v b p e", b=2, e=2), ACT.Copy)
-            words = half.bitcast(F32)
-            for vb in range(2):
-                nc.tensor.transpose(back[:, P * (2 * vb + u) : P * (2 * vb + u + 1)], words[:, P * vb : P * (vb + 1)], ident[:])
-
-        def copy_back(back, name):
-            dst = bf_tile(name, V * PACK)
-            nc.scalar.copy(dst[:].bitcast(F32).rearrange("p (b v u) -> p b v u", b=2, u=2),
-                           back[:].rearrange("p (b u v) -> p b v u", b=2, u=2))
-            return dst
+                mx(out_acc[m], w_q, slice(w0 + P * m, w0 + P * (m + 1)), v_q, slice(0, V), start, stop)
 
         W = N * PACK
+        ha, hc = f32_tile("ha"), f32_tile("hc")
+        for t in range(PACK):
+            gather(ha[:, t, :], t, ea_t[:], 2 * t < VECTOR_GATHERS)
+            gather(hc[:, t, :], t, ec_t[:], 2 * t + 1 < VECTOR_GATHERS)
+
         w43_bf = bf_tile("w43_bf", 2 * W)
         w65_bf = bf_tile("w65_bf", 2 * W)
         w2_bf = bf_tile("w2_bf", W)
-        interleave(w4_raw[:], w43_bf[:, 0:W], ACT.Copy)
-        interleave(w3_raw[:], w43_bf[:, W : 2 * W], ACT.Copy)
-        interleave(w6_raw[:], w65_bf[:, 0:W], ACT.Copy)
-        interleave(w5_raw[:], w65_bf[:, W : 2 * W], ACT.Copy)
-        interleave(w2_raw[:], w2_bf[:], ACT.Copy)
-
-        ha = f32_tile("ha")
-        hb = f32_tile("hb")
-        diff1 = f32_tile("diff1")
-        diff2 = f32_tile("diff2")
-        acc1, acc2 = banks[0:2], [banks[5], banks[2]]
-        for t in range(PACK):
-            nc.vector.tensor_copy(ha[:, t, :], h[t][:].indirect(ea_t[:]))
-            add_transposed(ha, t, acc1, 2, True, False)
-            nc.vector.tensor_copy(hb[:, t, :], h[t][:].indirect(eb_t[:]))
-            nc.vector.tensor_tensor(diff1[:, t, :], h[t][:].indirect(ec_t[:]), ha[:, t, :], ALU.subtract)
-            add_transposed(diff1, t, acc1, 1, False, True)
-            add_transposed(hb, t, acc2, 2, True, False)
-        stage = bf_tile("stage", 4 * W, "w2_raw")
-        d_bf, rows1, rows2 = stage[:, 0 : 2 * W], stage[:, 2 * W : 3 * W], stage[:, 3 * W : 4 * W]
-        turn_back(acc1, rows1, banks[3], 0)
-        interleave(diff1[:], d_bf[:, 0:W], ACT.Abs)
-        turn_back(acc1, rows1, banks[3], 1)
-        for t in range(PACK):
-            nc.vector.tensor_tensor(diff2[:, t, :], h[t][:].indirect(ed_t[:]), hb[:, t, :], ALU.subtract)
-            add_transposed(diff2, t, acc2, 1, False, True)
-        turn_back(acc2, rows2, banks[4], 0)
-        interleave(diff2[:], d_bf[:, W : 2 * W], ACT.Abs)
-        turn_back(acc2, rows2, banks[4], 1)
-        s1_bf = copy_back(banks[3], "s1_bf")
-        s2_bf = copy_back(banks[4], "s2_bf")
-
+        nc.vector.tensor_copy(woven(w43_bf[:, 0:W]), planes(w4_raw[:]))
+        nc.vector.tensor_copy(woven(w43_bf[:, W : 2 * W]), planes(w3_raw[:]))
+        nc.vector.tensor_copy(woven(w65_bf[:, 0:W]), planes(w6_raw[:]))
         w43_q = quantize(w43_bf[:], "w43")
+        nc.vector.tensor_copy(woven(w65_bf[:, W : 2 * W]), planes(w5_raw[:]))
+        nc.vector.tensor_copy(woven(w2_bf[:]), planes(w2_raw[:]))
         w65_q = quantize(w65_bf[:], "w65")
-        d_q = quantize(d_bf, "d")
-        product(w43_q, 0, d_q, 0, True)
-        product(w65_q, 0, d_q, V, False)
-        product(w43_q, N, quantize(s1_bf[:], "s1"), 0, False)
-        product(w65_q, N, quantize(s2_bf[:], "s2"), 0, False)
-        hown = keep.tile([P, 2 * PACK * P], F32, name="hown", tag="diff2", align_bytes=64)
-        own_bf = []
-        for vb in range(2):
-            half = hown[:, PACK * P * vb : PACK * P * (vb + 1)].rearrange("p (t v) -> p t v", t=PACK)
-            for t in range(PACK):
-                nc.vector.tensor_copy(half[:, t, :], h[t][:].indirect(own_t[:, 8 * vb : 8 * (vb + 1)]))
-            own_bf.append(bf_tile(f"own_bf{vb}", PACK * P))
-            if vb == 0:
-                interleave(half, own_bf[vb][:], ACT.Copy)
-            else:
-                interleave(half[:, :, 0:64], own_bf[vb][:, 0:256], ACT.Copy)
-                nc.vector.tensor_copy(own_bf[vb][:, 256:512].rearrange("p (c i t) -> p c t i", i=LINE, t=PACK),
-                                      half[:, :, 64:128].rearrange("p t (c i) -> p c t i", i=LINE))
-        w2_q = quantize(w2_bf[:], "w2", "h0")
-        for vb in range(2):
-            half_product(w2_q, 0, quantize(own_bf[vb][:], f"own{vb}"), 0, vb, False, True)
-            res = keep.tile([P, 2, P], F32, name=f"res{vb}")
-            nc.scalar.activation(res[:, 0, :], out_acc[vb][0], ACT.Copy)
-            if vb == 0:
-                nc.scalar.activation(res[:, 1, :], out_acc[vb][1], ACT.Copy)
-            else:
-                nc.vector.tensor_copy(res[:, 1, :], out_acc[vb][1])
-            nc.sync.dma_start(out[:, P * vb : P * (vb + 1)].rearrange("(m p) v -> p m v", m=2), res[:])
+        w2_q = quantize(w2_bf[:], "w2")
+
+        hb, hd = f32_tile("hb", "w1_3_codes"), f32_tile("hd", "w1_3_scale")
+        for t in range(PACK):
+            gather(hb[:, t, :], t, eb_t[:], False)
+            gather(hd[:, t, :], t, ed_t[:], False)
+
+        def pair(first, second, name, slots):
+            signed, total = bf_tile(name + "_signed", W, slots[0]), bf_tile(name + "_sum", W, slots[1])
+            nc.vector.tensor_tensor(woven(signed[:]), planes(first[:]), planes(second[:]), ALU.subtract)
+            nc.vector.tensor_tensor(woven(total[:]), planes(first[:]), planes(second[:]), ALU.add)
+            return signed, total
+
+        signed1, s1_bf = pair(ha, hc, "ac", ("w2_raw", "w5_raw"))
+        negated1, d1_bf = bf_tile("negated1", W), bf_tile("d1_bf", W)
+        nc.vector.tensor_scalar(negated1[:], signed1[:], -1.0, None, ALU.mult)
+        product(w43_q, N, quantize(s1_bf[:], "s1"), True, False)
+        nc.vector.tensor_tensor(d1_bf[:], signed1[:], negated1[:], ALU.max)
+        hown = f32_tile("hown", "ha")
+        for t in range(PACK):
+            gather(hown[:, t, :], t, own_t[:], False)
+        signed2, s2_bf = pair(hb, hd, "bd", ("negated1", "hc"))
+        product(w43_q, 0, quantize(d1_bf[:], "d1"), False, False)
+        product(w65_q, N, quantize(s2_bf[:], "s2"), False, False)
+        own_bf, d2_bf = bf_tile("own_bf", W), bf_tile("d2_bf", W)
+        nc.vector.tensor_copy(woven(own_bf[:]), planes(hown[:]))
+        nc.scalar.activation(d2_bf[:], signed2[:], ACT.Abs)
+        product(w2_q, 0, quantize(own_bf[:], "own"), False, False)
+        product(w65_q, 0, quantize(d2_bf[:], "d2"), False, True)
+        res = [keep.tile([P, V], F32, name=f"res{m}") for m in range(2)]
+        nc.scalar.activation(res[0][:], out_acc[0], ACT.Copy)
+        nc.sync.dma_start(out[0:P, :], res[0][:])
+        nc.vector.tensor_copy(res[1][:], out_acc[1])
+        nc.scalar.dma_start(out[P : 2 * P, :], res[1][:])

@@ -1,6 +1,7 @@
 from contextlib import ExitStack
 
 import concourse.mybir as mybir
+from concourse.masks import make_identity
 
 K, T, S, H, N, V = 512, 2048, 512, 512, 256, 256
 FLOPS = 2 * K * H * S + 5 * 2 * H * N * V
@@ -19,7 +20,6 @@ P = 128
 PACK = 4
 LINE = 4
 W1_SCALAR_M = 24
-VECTOR_GATHERS = 3
 
 
 def tile_picked_ymeshcnn_lin_p_kernel(
@@ -88,6 +88,8 @@ def tile_picked_ymeshcnn_lin_p_kernel(
                 rhs=rhs[0][:, rcols].bitcast(FP8X4), rhs_scale=rhs[1][:, rcols], start=start, stop=stop)
 
         banks = [psum.tile([P, 512], F32, name=f"bank{b}") for b in range(7)]
+        ident = keep.tile([P, P], F32, name="ident")
+        make_identity(nc, ident[:])
         h = []
         for t in range(PACK):
             w1_q = quantize(w1_bf[:, t, :, :].rearrange("p m j -> p (m j)"), f"w1_{t}")
@@ -101,7 +103,10 @@ def tile_picked_ymeshcnn_lin_p_kernel(
             else:
                 acc = banks[1 + t][:]
                 mx(acc, w1_q, slice(0, P), (x_codes, x_scale), slice(0, S), True, True)
-                nc.scalar.activation(h_t[:], acc, ACT.Copy)
+                if t < PACK - 1:
+                    nc.scalar.activation(h_t[:], acc, ACT.Copy)
+                else:
+                    nc.vector.tensor_copy(h_t[:], acc)
             h.append(h_t)
 
         def woven(dst):
@@ -122,57 +127,96 @@ def tile_picked_ymeshcnn_lin_p_kernel(
             else:
                 nc.scalar.activation(dst, h[t][:].indirect(places), ACT.Copy)
 
+        def gather_negated(dst, t, places):
+            nc.scalar.activation(dst, h[t][:].indirect(places), ACT.Copy, scale=-1.0)
+
         out_acc = [banks[5][:, 0:V], banks[6][:, 0:V]]
 
-        def product(w_q, w0, v_q, start, stop):
+        def product(w_q, w0, v_q, start):
             for m in range(2):
-                mx(out_acc[m], w_q, slice(w0 + P * m, w0 + P * (m + 1)), v_q, slice(0, V), start, stop)
+                mx(out_acc[m], w_q, slice(w0 + P * m, w0 + P * (m + 1)), v_q, slice(0, V), start, False)
+
+        def add_transposed(src, t, acc, first):
+            for vb in range(2):
+                at = P * (2 * vb + t % 2)
+                nc.tensor.matmul(acc[t // 2][:, at : at + P], src[:, t, P * vb : P * (vb + 1)], ident[:],
+                                 start=(first and t % 2 == 0 and vb == 0),
+                                 stop=(not first and t % 2 == 1 and vb == 1), is_transpose=True)
+
+        def turn_back(acc, name, back, u):
+            half = bf_tile(f"{name}_{u}", 512)[:]
+            nc.scalar.activation(half.rearrange("v (b p e) -> v b p e", b=2, e=2),
+                                 acc[u][:].rearrange("v (b e p) -> v b p e", b=2, e=2), ACT.Abs)
+            words = half.bitcast(F32)
+            for vb in range(2):
+                nc.tensor.transpose(back[:, P * (2 * vb + u) : P * (2 * vb + u + 1)], words[:, P * vb : P * (vb + 1)], ident[:])
+
+        def copy_back(back, name, slot):
+            dst = bf_tile(name, V * PACK, slot)
+            nc.vector.tensor_copy(dst[:].bitcast(F32).rearrange("p (b v u) -> p b v u", b=2, u=2),
+                                  back[:].rearrange("p (b u v) -> p b v u", b=2, u=2))
+            return dst
 
         W = N * PACK
         ha, hc = f32_tile("ha"), f32_tile("hc")
+        acc1, acc2 = banks[0:2], banks[5:7]
         for t in range(PACK):
-            gather(ha[:, t, :], t, ea_t[:], 2 * t < VECTOR_GATHERS)
-            gather(hc[:, t, :], t, ec_t[:], 2 * t + 1 < VECTOR_GATHERS)
+            gather(ha[:, t, :], t, ea_t[:], True)
+            gather_negated(hc[:, t, :], t, ec_t[:])
+            add_transposed(ha, t, acc1, True)
+            add_transposed(hc, t, acc1, False)
+        turn_back(acc1, "rows1", banks[3], 0)
+        turn_back(acc1, "rows1", banks[3], 1)
 
         w43_bf = bf_tile("w43_bf", 2 * W)
         w65_bf = bf_tile("w65_bf", 2 * W)
         w2_bf = bf_tile("w2_bf", W)
-        nc.vector.tensor_copy(woven(w43_bf[:, 0:W]), planes(w4_raw[:]))
-        nc.vector.tensor_copy(woven(w43_bf[:, W : 2 * W]), planes(w3_raw[:]))
-        nc.vector.tensor_copy(woven(w65_bf[:, 0:W]), planes(w6_raw[:]))
+
+        def cast_weight(dst, raw):
+            nc.gpsimd.tensor_scalar(dst.rearrange("p (c t) -> p c t", t=PACK), raw.rearrange("p t c -> p c t"),
+                                    1.0, 0.0, ALU.mult, ALU.add)
+
+        cast_weight(w43_bf[:, 0:W], w4_raw[:])
+        cast_weight(w43_bf[:, W : 2 * W], w3_raw[:])
+        cast_weight(w65_bf[:, 0:W], w6_raw[:])
+        cast_weight(w65_bf[:, W : 2 * W], w5_raw[:])
+        cast_weight(w2_bf[:], w2_raw[:])
         w43_q = quantize(w43_bf[:], "w43")
-        nc.vector.tensor_copy(woven(w65_bf[:, W : 2 * W]), planes(w5_raw[:]))
-        nc.vector.tensor_copy(woven(w2_bf[:]), planes(w2_raw[:]))
         w65_q = quantize(w65_bf[:], "w65")
         w2_q = quantize(w2_bf[:], "w2")
 
-        hb, hd = f32_tile("hb", "w1_3_codes"), f32_tile("hd", "w1_3_scale")
+        hb, hd = f32_tile("hb", "w1_3_codes"), f32_tile("hd", "rows1_0")
         for t in range(PACK):
-            gather(hb[:, t, :], t, eb_t[:], False)
-            gather(hd[:, t, :], t, ed_t[:], False)
+            gather_negated(hd[:, t, :], t, ed_t[:])
+            gather(hb[:, t, :], t, eb_t[:], t < PACK - 1)
+            add_transposed(hd, t, acc2, True)
+            add_transposed(hb, t, acc2, False)
+        turn_back(acc2, "rows2", banks[4], 0)
+        turn_back(acc2, "rows2", banks[4], 1)
 
-        def pair(first, second, name, slots):
-            signed, total = bf_tile(name + "_signed", W, slots[0]), bf_tile(name + "_sum", W, slots[1])
-            nc.vector.tensor_tensor(woven(signed[:]), planes(first[:]), planes(second[:]), ALU.subtract)
-            nc.vector.tensor_tensor(woven(total[:]), planes(first[:]), planes(second[:]), ALU.add)
-            return signed, total
+        def total(first, negated, name, slot):
+            dst = bf_tile(name, W, slot)
+            nc.vector.tensor_tensor(woven(dst[:]), planes(first[:]), planes(negated[:]), ALU.subtract)
+            return dst
 
-        signed1, s1_bf = pair(ha, hc, "ac", ("w2_raw", "w5_raw"))
-        negated1, d1_bf = bf_tile("negated1", W), bf_tile("d1_bf", W)
-        nc.vector.tensor_scalar(negated1[:], signed1[:], -1.0, None, ALU.mult)
-        product(w43_q, N, quantize(s1_bf[:], "s1"), True, False)
-        nc.vector.tensor_tensor(d1_bf[:], signed1[:], negated1[:], ALU.max)
-        hown = f32_tile("hown", "ha")
-        for t in range(PACK):
-            gather(hown[:, t, :], t, own_t[:], False)
-        signed2, s2_bf = pair(hb, hd, "bd", ("negated1", "hc"))
-        product(w43_q, 0, quantize(d1_bf[:], "d1"), False, False)
-        product(w65_q, N, quantize(s2_bf[:], "s2"), False, False)
-        own_bf, d2_bf = bf_tile("own_bf", W), bf_tile("d2_bf", W)
-        nc.vector.tensor_copy(woven(own_bf[:]), planes(hown[:]))
-        nc.scalar.activation(d2_bf[:], signed2[:], ACT.Abs)
-        product(w2_q, 0, quantize(own_bf[:], "own"), False, False)
-        product(w65_q, 0, quantize(d2_bf[:], "d2"), False, True)
+        s1_bf = total(ha, hc, "s1_bf", None)
+        d1_bf = copy_back(banks[3], "d1_bf", None)
+        product(w43_q, N, quantize(s1_bf[:], "s1"), True)
+        product(w43_q, 0, quantize(d1_bf[:], "d1"), False)
+        s2_bf = total(hb, hd, "s2_bf", "d1_bf")
+        d2_bf = copy_back(banks[4], "d2_bf", "w2_bf")
+        product(w65_q, N, quantize(s2_bf[:], "s2"), False)
+        product(w65_q, 0, quantize(d2_bf[:], "d2"), False)
+        hown = keep.tile([P, 2 * PACK * P], F32, name="hown", tag="rows2_0", align_bytes=64)
+        for vb in range(2):
+            half = hown[:, PACK * P * vb : PACK * P * (vb + 1)].rearrange("p (t v) -> p t v", t=PACK)
+            for t in range(PACK):
+                gather(half[:, t, :], t, own_t[:, 8 * vb : 8 * (vb + 1)], False)
+            own_bf = bf_tile(f"own_bf{vb}", PACK * P, ("rows1_0", "w1_3_codes")[vb])
+            nc.vector.tensor_copy(woven(own_bf[:]), planes(half))
+            own_q = quantize(own_bf[:], f"own{vb}")
+            for m in range(2):
+                mx(out_acc[m][:, P * vb : P * (vb + 1)], w2_q, slice(P * m, P * (m + 1)), own_q, slice(0, P), False, vb == 1)
         res = [keep.tile([P, V], F32, name=f"res{m}") for m in range(2)]
         nc.scalar.activation(res[0][:], out_acc[0], ACT.Copy)
         nc.sync.dma_start(out[0:P, :], res[0][:])

@@ -75,9 +75,9 @@ def tile_picked_ymeshcnn_lin_p_kernel(
         nc.scalar.activation(*w1_views(1, 0, W1_SCALAR_M), ACT.Copy)
         nc.vector.tensor_copy(*w1_views(1, W1_SCALAR_M, 64))
 
-        def quantize(src, name):
+        def quantize(src, name, slot=None):
             width = src.shape[1] // PACK
-            codes = keep.tile([P, width], U32, name=name + "_codes", align_bytes=64)
+            codes = keep.tile([P, width], U32, name=name + "_codes", tag=slot or name + "_codes", align_bytes=64)
             scale = keep.tile([P, width], U8, name=name + "_scale", align_bytes=64)
             nc.vector.quantize_mx(out=codes[:].bitcast(FP8X4), scales=scale[:], in_=src)
             return codes, scale
@@ -99,7 +99,7 @@ def tile_picked_ymeshcnn_lin_p_kernel(
                     cols = slice(256 * u, 256 * (u + 1))
                     acc = banks[u][:, 0:256]
                     mx(acc, w1_q, slice(0, P), (x_codes, x_scale), cols, True, True)
-                    nc.vector.tensor_copy(h_t[:, cols], acc)
+                    nc.scalar.activation(h_t[:, cols], acc, ACT.Copy)
             else:
                 acc = banks[1 + t][:]
                 mx(acc, w1_q, slice(0, P), (x_codes, x_scale), slice(0, S), True, True)
@@ -168,7 +168,8 @@ def tile_picked_ymeshcnn_lin_p_kernel(
         turn_back(acc1, "rows1", banks[3], 0)
         turn_back(acc1, "rows1", banks[3], 1)
 
-        w43_bf = bf_tile("w43_bf", 2 * W)
+        w4_bf = bf_tile("w4_bf", W, "w1_bf")
+        w3_bf = bf_tile("w3_bf", W, "w4_raw")
         w65_bf = bf_tile("w65_bf", 2 * W)
         w2_bf = bf_tile("w2_bf", W)
 
@@ -176,19 +177,20 @@ def tile_picked_ymeshcnn_lin_p_kernel(
             nc.gpsimd.tensor_scalar(dst.rearrange("p (c t) -> p c t", t=PACK), raw.rearrange("p t c -> p c t"),
                                     1.0, 0.0, ALU.mult, ALU.add)
 
-        cast_weight(w43_bf[:, 0:W], w4_raw[:])
-        cast_weight(w43_bf[:, W : 2 * W], w3_raw[:])
+        nc.vector.tensor_copy(woven(w4_bf[:]), planes(w4_raw[:]))
+        cast_weight(w3_bf[:], w3_raw[:])
         cast_weight(w65_bf[:, 0:W], w6_raw[:])
         cast_weight(w65_bf[:, W : 2 * W], w5_raw[:])
         cast_weight(w2_bf[:], w2_raw[:])
-        w43_q = quantize(w43_bf[:], "w43")
+        w4_q = quantize(w4_bf[:], "w4", "w2_raw")
+        w3_q = quantize(w3_bf[:], "w3", "w5_raw")
         w65_q = quantize(w65_bf[:], "w65")
         w2_q = quantize(w2_bf[:], "w2")
 
         hb, hd = f32_tile("hb", "w1_3_codes"), f32_tile("hd", "rows1_0")
         for t in range(PACK):
             gather_negated(hd[:, t, :], t, ed_t[:])
-            gather(hb[:, t, :], t, eb_t[:], t < PACK - 1)
+            gather(hb[:, t, :], t, eb_t[:], True)
             add_transposed(hd, t, acc2, True)
             add_transposed(hb, t, acc2, False)
         turn_back(acc2, "rows2", banks[4], 0)
@@ -201,8 +203,8 @@ def tile_picked_ymeshcnn_lin_p_kernel(
 
         s1_bf = total(ha, hc, "s1_bf", None)
         d1_bf = copy_back(banks[3], "d1_bf", None)
-        product(w43_q, N, quantize(s1_bf[:], "s1"), True)
-        product(w43_q, 0, quantize(d1_bf[:], "d1"), False)
+        product(w3_q, 0, quantize(s1_bf[:], "s1"), True)
+        product(w4_q, 0, quantize(d1_bf[:], "d1"), False)
         s2_bf = total(hb, hd, "s2_bf", "d1_bf")
         d2_bf = copy_back(banks[4], "d2_bf", "w2_bf")
         product(w65_q, N, quantize(s2_bf[:], "s2"), False)

@@ -19,7 +19,8 @@ ACT = mybir.ActivationFunctionType
 P = 128
 PACK = 4
 LINE = 4
-W1_SCALAR_M = 24
+W1_SCALAR_M = 64
+VECTOR_B_PLANES = 1
 
 
 def tile_picked_ymeshcnn_lin_p_kernel(
@@ -43,11 +44,11 @@ def tile_picked_ymeshcnn_lin_p_kernel(
         xs_all = keep.tile([P, T], U8, name="xs_all")
         nc.vector.memset(xs_all[:].bitcast(I32), 0)
         offs_t = load_list(offs, "offs_t")
-        xw_all = keep.tile([P, T], U32, name="xw_all")
-        nc.sync.dma_start(xw_all[:].bitcast(I32), x_words[0].rearrange("p n t -> p (n t)").bitcast(I32))
+        w1_raw = load_weight(w1, "w1_raw")
         for q in range(4):
             nc.sync.dma_start(xs_all[32 * q : 32 * q + 4, :].bitcast(I32), x_scales[0, 4 * q : 4 * q + 4, :].bitcast(I32))
-        w1_raw = [load_weight(w1[:, u * 256 : (u + 1) * 256], f"w1_raw{u}") for u in range(2)]
+        xw_all = keep.tile([P, T], U32, name="xw_all")
+        nc.sync.dma_start(xw_all[:].bitcast(I32), x_words[0].rearrange("p n t -> p (n t)").bitcast(I32))
         ea_t = load_list(ea, "ea_t")
         ec_t = load_list(ec, "ec_t")
         w4_raw = load_weight(w4, "w4_raw")
@@ -59,21 +60,15 @@ def tile_picked_ymeshcnn_lin_p_kernel(
         w5_raw = load_weight(w5, "w5_raw")
         w2_raw = load_weight(w2, "w2_raw")
 
-        x_codes = keep.tile([P, S], U32, name="x_codes", align_bytes=64)
-        x_scale = keep.tile([P, S], U8, name="x_scale", align_bytes=64)
-        nc.vector.tensor_copy(x_scale[:], xs_all[:].indirect(offs_t[:]))
-        nc.vector.tensor_copy(x_codes[:], xw_all[:].indirect(offs_t[:]))
-
         w1_bf = keep.tile([P, PACK, P, PACK], BF16, name="w1_bf", align_bytes=64)
 
-        def w1_views(u, m0, m1):
-            dst = w1_bf[:, :, 64 * u + m0 : 64 * u + m1, :].rearrange("p t m j -> p m j t")
-            src = w1_raw[u][:, :, PACK * m0 : PACK * m1].rearrange("p j (m t) -> p m j t", t=PACK)
+        def w1_views(m0, m1):
+            dst = w1_bf[:, :, m0:m1, :].rearrange("p t m j -> p m j t")
+            src = w1_raw[:, :, PACK * m0 : PACK * m1].rearrange("p j (m t) -> p m j t", t=PACK)
             return dst, src
 
-        nc.scalar.activation(*w1_views(0, 0, 64), ACT.Copy)
-        nc.scalar.activation(*w1_views(1, 0, W1_SCALAR_M), ACT.Copy)
-        nc.vector.tensor_copy(*w1_views(1, W1_SCALAR_M, 64))
+        nc.scalar.activation(*w1_views(0, W1_SCALAR_M), ACT.Copy)
+        nc.vector.tensor_copy(*w1_views(W1_SCALAR_M, P))
 
         def quantize(src, name, slot=None):
             width = src.shape[1] // PACK
@@ -87,27 +82,33 @@ def tile_picked_ymeshcnn_lin_p_kernel(
                 out=acc, lhsT=lhs[0][:, lcols].bitcast(FP8X4), lhsT_scale=lhs[1][:, lcols],
                 rhs=rhs[0][:, rcols].bitcast(FP8X4), rhs_scale=rhs[1][:, rcols], start=start, stop=stop)
 
-        banks = [psum.tile([P, 512], F32, name=f"bank{b}") for b in range(7)]
+        banks = [psum.tile([P, 512], F32, name=f"bank{b}") for b in range(8)]
         ident = keep.tile([P, P], F32, name="ident")
         make_identity(nc, ident[:])
-        h = []
-        for t in range(PACK):
-            w1_q = quantize(w1_bf[:, t, :, :].rearrange("p m j -> p (m j)"), f"w1_{t}")
-            h_t = keep.tile([P, S], F32, name=f"h{t}", align_bytes=64)
-            if t == 0:
-                for u in range(2):
-                    cols = slice(256 * u, 256 * (u + 1))
-                    acc = banks[u][:, 0:256]
-                    mx(acc, w1_q, slice(0, P), (x_codes, x_scale), cols, True, True)
-                    nc.scalar.activation(h_t[:, cols], acc, ACT.Copy)
-            else:
-                acc = banks[1 + t][:]
-                mx(acc, w1_q, slice(0, P), (x_codes, x_scale), slice(0, S), True, True)
-                if t < PACK - 1:
-                    nc.scalar.activation(h_t[:], acc, ACT.Copy)
-                else:
-                    nc.vector.tensor_copy(h_t[:], acc)
-            h.append(h_t)
+        x_scale = keep.tile([P, S], U8, name="x_scale", align_bytes=64)
+        nc.vector.tensor_copy(x_scale[:], xs_all[:].indirect(offs_t[:]))
+        w1_q = quantize(w1_bf[:].rearrange("p t m j -> p (t m j)"), "w1")
+        halves = [slice(0, S // 2), slice(S // 2, S)]
+        x_codes = [keep.tile([P, S // 2], U32, name=f"x_codes{u}", align_bytes=64) for u in range(2)]
+        for u in range(2):
+            nc.vector.tensor_copy(x_codes[u][:], xw_all[:].indirect(offs_t[:, 16 * u : 16 * (u + 1)]))
+        h = [keep.tile([P, S], F32, name=f"h{t}", align_bytes=64) for t in range(PACK)]
+
+        def first_layer(acc, t, u):
+            nc.tensor.matmul_mx(
+                out=acc, lhsT=w1_q[0][:, P * t : P * (t + 1)].bitcast(FP8X4), lhsT_scale=w1_q[1][:, P * t : P * (t + 1)],
+                rhs=x_codes[u][:].bitcast(FP8X4), rhs_scale=x_scale[:, halves[u]], start=True, stop=True)
+
+        for u in range(2):
+            for t in range(2):
+                acc = banks[(0, 2, 1, 7)[2 * u + t]][:, 0 : S // 2]
+                first_layer(acc, t, u)
+                nc.scalar.activation(h[t][:, halves[u]], acc, ACT.Copy)
+        for t in range(2, PACK):
+            for u in range(2):
+                first_layer(banks[1 + t][:, halves[u]], t, u)
+        nc.scalar.activation(h[2][:], banks[3][:], ACT.Copy)
+        nc.vector.tensor_copy(h[3][:], banks[4][:])
 
         def woven(dst):
             return dst.rearrange("p (c i t) -> p c t i", i=LINE, t=PACK)
@@ -130,11 +131,15 @@ def tile_picked_ymeshcnn_lin_p_kernel(
         def gather_negated(dst, t, places):
             nc.scalar.activation(dst, h[t][:].indirect(places), ACT.Copy, scale=-1.0)
 
-        out_acc = [banks[5][:, 0:V], banks[6][:, 0:V]]
+        out_acc = [[banks[5][:, 0:P], banks[6][:, 0:P]], [banks[0][:, 0:P], banks[1][:, 0:P]]]
 
-        def product(w_q, w0, v_q, start):
+        def half_product(w_q, w0, v_q, v0, vb, start, stop):
             for m in range(2):
-                mx(out_acc[m], w_q, slice(w0 + P * m, w0 + P * (m + 1)), v_q, slice(0, V), start, False)
+                mx(out_acc[vb][m], w_q, slice(w0 + P * m, w0 + P * (m + 1)), v_q, slice(v0, v0 + P), start, stop)
+
+        def product(w_q, w0, v_q, v0, start):
+            for vb in range(2):
+                half_product(w_q, w0, v_q, v0 + P * vb, vb, start, False)
 
         def add_transposed(src, t, acc, first):
             for vb in range(2):
@@ -151,11 +156,9 @@ def tile_picked_ymeshcnn_lin_p_kernel(
             for vb in range(2):
                 nc.tensor.transpose(back[:, P * (2 * vb + u) : P * (2 * vb + u + 1)], words[:, P * vb : P * (vb + 1)], ident[:])
 
-        def copy_back(back, name, slot):
-            dst = bf_tile(name, V * PACK, slot)
-            nc.vector.tensor_copy(dst[:].bitcast(F32).rearrange("p (b v u) -> p b v u", b=2, u=2),
+        def copy_back(dst, back):
+            nc.vector.tensor_copy(dst.bitcast(F32).rearrange("p (b v u) -> p b v u", b=2, u=2),
                                   back[:].rearrange("p (b u v) -> p b v u", b=2, u=2))
-            return dst
 
         W = N * PACK
         ha, hc = f32_tile("ha"), f32_tile("hc")
@@ -168,59 +171,55 @@ def tile_picked_ymeshcnn_lin_p_kernel(
         turn_back(acc1, "rows1", banks[3], 0)
         turn_back(acc1, "rows1", banks[3], 1)
 
-        w4_bf = bf_tile("w4_bf", W, "w1_bf")
-        w3_bf = bf_tile("w3_bf", W, "w4_raw")
+        w43_bf = bf_tile("w43_bf", 2 * W)
         w65_bf = bf_tile("w65_bf", 2 * W)
         w2_bf = bf_tile("w2_bf", W)
-
-        def cast_weight(dst, raw):
-            nc.gpsimd.tensor_scalar(dst.rearrange("p (c t) -> p c t", t=PACK), raw.rearrange("p t c -> p c t"),
-                                    1.0, 0.0, ALU.mult, ALU.add)
-
-        nc.vector.tensor_copy(woven(w4_bf[:]), planes(w4_raw[:]))
-        cast_weight(w3_bf[:], w3_raw[:])
-        cast_weight(w65_bf[:, 0:W], w6_raw[:])
-        cast_weight(w65_bf[:, W : 2 * W], w5_raw[:])
-        cast_weight(w2_bf[:], w2_raw[:])
-        w4_q = quantize(w4_bf[:], "w4", "w2_raw")
-        w3_q = quantize(w3_bf[:], "w3", "w5_raw")
+        nc.vector.tensor_copy(woven(w43_bf[:, 0:W]), planes(w4_raw[:]))
+        nc.vector.tensor_copy(woven(w43_bf[:, W : 2 * W]), planes(w3_raw[:]))
+        nc.vector.tensor_copy(woven(w65_bf[:, 0:W]), planes(w6_raw[:]))
+        w43_q = quantize(w43_bf[:], "w43")
+        nc.vector.tensor_copy(woven(w65_bf[:, W : 2 * W]), planes(w5_raw[:]))
+        nc.vector.tensor_copy(woven(w2_bf[:]), planes(w2_raw[:]))
         w65_q = quantize(w65_bf[:], "w65")
         w2_q = quantize(w2_bf[:], "w2")
 
-        hb, hd = f32_tile("hb", "w1_3_codes"), f32_tile("hd", "rows1_0")
+        hb, hd = f32_tile("hb", "w1_codes"), f32_tile("hd", "rows1_0")
         for t in range(PACK):
             gather_negated(hd[:, t, :], t, ed_t[:])
-            gather(hb[:, t, :], t, eb_t[:], True)
+            gather(hb[:, t, :], t, eb_t[:], t < VECTOR_B_PLANES)
             add_transposed(hd, t, acc2, True)
             add_transposed(hb, t, acc2, False)
         turn_back(acc2, "rows2", banks[4], 0)
         turn_back(acc2, "rows2", banks[4], 1)
 
-        def total(first, negated, name, slot):
-            dst = bf_tile(name, W, slot)
-            nc.vector.tensor_tensor(woven(dst[:]), planes(first[:]), planes(negated[:]), ALU.subtract)
-            return dst
+        def total(dst, first, negated):
+            nc.vector.tensor_tensor(woven(dst), planes(first[:]), planes(negated[:]), ALU.subtract)
 
-        s1_bf = total(ha, hc, "s1_bf", None)
-        d1_bf = copy_back(banks[3], "d1_bf", None)
-        product(w3_q, 0, quantize(s1_bf[:], "s1"), True)
-        product(w4_q, 0, quantize(d1_bf[:], "d1"), False)
-        s2_bf = total(hb, hd, "s2_bf", "d1_bf")
-        d2_bf = copy_back(banks[4], "d2_bf", "w2_bf")
-        product(w65_q, N, quantize(s2_bf[:], "s2"), False)
-        product(w65_q, 0, quantize(d2_bf[:], "d2"), False)
+        ds1_bf = bf_tile("ds1_bf", 2 * W, "w2_raw")
+        total(ds1_bf[:, W : 2 * W], ha, hc)
+        copy_back(ds1_bf[:, 0:W], banks[3])
+        ds1_q = quantize(ds1_bf[:], "ds1")
+        product(w43_q, 0, ds1_q, 0, True)
+        product(w43_q, N, ds1_q, V, False)
+        s2_bf = bf_tile("s2_bf", W, "ha")
+        d2_bf = bf_tile("d2_bf", W, "w2_raw")
+        total(s2_bf[:], hb, hd)
+        s2_q = quantize(s2_bf[:], "s2")
+        copy_back(d2_bf[:], banks[4])
+        product(w65_q, N, s2_q, 0, False)
+        product(w65_q, 0, quantize(d2_bf[:], "d2"), 0, False)
         hown = keep.tile([P, 2 * PACK * P], F32, name="hown", tag="rows2_0", align_bytes=64)
         for vb in range(2):
             half = hown[:, PACK * P * vb : PACK * P * (vb + 1)].rearrange("p (t v) -> p t v", t=PACK)
             for t in range(PACK):
                 gather(half[:, t, :], t, own_t[:, 8 * vb : 8 * (vb + 1)], False)
-            own_bf = bf_tile(f"own_bf{vb}", PACK * P, ("rows1_0", "w1_3_codes")[vb])
+            own_bf = bf_tile(f"own_bf{vb}", PACK * P, ("rows1_0", "w1_codes")[vb])
             nc.vector.tensor_copy(woven(own_bf[:]), planes(half))
-            own_q = quantize(own_bf[:], f"own{vb}")
-            for m in range(2):
-                mx(out_acc[m][:, P * vb : P * (vb + 1)], w2_q, slice(P * m, P * (m + 1)), own_q, slice(0, P), False, vb == 1)
-        res = [keep.tile([P, V], F32, name=f"res{m}") for m in range(2)]
-        nc.scalar.activation(res[0][:], out_acc[0], ACT.Copy)
-        nc.sync.dma_start(out[0:P, :], res[0][:])
-        nc.vector.tensor_copy(res[1][:], out_acc[1])
-        nc.scalar.dma_start(out[P : 2 * P, :], res[1][:])
+            half_product(w2_q, 0, quantize(own_bf[:], f"own{vb}"), 0, vb, False, True)
+            res = keep.tile([P, 2, P], F32, name=f"res{vb}")
+            nc.scalar.activation(res[:, 0, :], out_acc[vb][0], ACT.Copy)
+            if vb == 0:
+                nc.scalar.activation(res[:, 1, :], out_acc[vb][1], ACT.Copy)
+            else:
+                nc.vector.tensor_copy(res[:, 1, :], out_acc[vb][1])
+            nc.sync.dma_start(out[:, P * vb : P * (vb + 1)].rearrange("(m p) v -> p m v", m=2), res[:])

@@ -18,9 +18,8 @@ ACT = mybir.ActivationFunctionType
 
 P = 128
 PACK = 4
-LINE = 4
+LINE = 2
 W1_SCALAR_M = 64
-VECTOR_B_PLANES = 1
 
 
 def tile_picked_ymeshcnn_lin_p_kernel(
@@ -186,7 +185,11 @@ def tile_picked_ymeshcnn_lin_p_kernel(
         hb, hd = f32_tile("hb", "w1_codes"), f32_tile("hd", "rows1_0")
         for t in range(PACK):
             gather_negated(hd[:, t, :], t, ed_t[:])
-            gather(hb[:, t, :], t, eb_t[:], t < VECTOR_B_PLANES)
+            if t == 0:
+                gather(hb[:, t, 0:P], t, eb_t[:, 0:8], True)
+                gather(hb[:, t, P:V], t, eb_t[:, 8:16], False)
+            else:
+                gather(hb[:, t, :], t, eb_t[:], False)
             add_transposed(hd, t, acc2, True)
             add_transposed(hb, t, acc2, False)
         turn_back(acc2, "rows2", banks[4], 0)

@@ -53,11 +53,11 @@ def tile_picked_ymeshcnn_lin_p_kernel(
         w4_raw = load_weight(w4, "w4_raw")
         w3_raw = load_weight(w3, "w3_raw")
         eb_t = load_list(eb, "eb_t")
-        ed_t = load_list(ed, "ed_t")
-        own_t = load_list(own, "own_t")
         w6_raw = load_weight(w6, "w6_raw")
+        ed_t = load_list(ed, "ed_t")
         w5_raw = load_weight(w5, "w5_raw")
         w2_raw = load_weight(w2, "w2_raw")
+        own_t = load_list(own, "own_t")
 
         w1_bf = keep.tile([P, PACK, P, PACK], BF16, name="w1_bf", align_bytes=64)
 
@@ -182,16 +182,17 @@ def tile_picked_ymeshcnn_lin_p_kernel(
         w65_q = quantize(w65_bf[:], "w65")
         w2_q = quantize(w2_bf[:], "w2")
 
-        hb, hd = f32_tile("hb", "w1_codes"), f32_tile("hd", "rows1_0")
+        hb, hd = f32_tile("hb", "w1_codes"), f32_tile("hd")
         for t in range(PACK):
-            gather_negated(hd[:, t, :], t, ed_t[:])
             if t == 0:
                 gather(hb[:, t, 0:P], t, eb_t[:, 0:8], True)
                 gather(hb[:, t, P:V], t, eb_t[:, 8:16], False)
             else:
                 gather(hb[:, t, :], t, eb_t[:], False)
-            add_transposed(hd, t, acc2, True)
-            add_transposed(hb, t, acc2, False)
+            add_transposed(hb, t, acc2, True)
+        for t in range(PACK):
+            gather_negated(hd[:, t, :], t, ed_t[:])
+            add_transposed(hd, t, acc2, False)
         turn_back(acc2, "rows2", banks[4], 0)
         turn_back(acc2, "rows2", banks[4], 1)
 
@@ -211,12 +212,12 @@ def tile_picked_ymeshcnn_lin_p_kernel(
         copy_back(d2_bf[:], banks[4])
         product(w65_q, N, s2_q, 0, False)
         product(w65_q, 0, quantize(d2_bf[:], "d2"), 0, False)
-        hown = keep.tile([P, 2 * PACK * P], F32, name="hown", tag="rows2_0", align_bytes=64)
+        hown = keep.tile([P, 2 * PACK * P], F32, name="hown", align_bytes=64)
         for vb in range(2):
             half = hown[:, PACK * P * vb : PACK * P * (vb + 1)].rearrange("p (t v) -> p t v", t=PACK)
             for t in range(PACK):
                 gather(half[:, t, :], t, own_t[:, 8 * vb : 8 * (vb + 1)], False)
-            own_bf = bf_tile(f"own_bf{vb}", PACK * P, ("rows1_0", "w1_codes")[vb])
+            own_bf = bf_tile(f"own_bf{vb}", PACK * P, ("hd", "w1_codes")[vb])
             nc.vector.tensor_copy(woven(own_bf[:]), planes(half))
             half_product(w2_q, 0, quantize(own_bf[:], f"own{vb}"), 0, vb, False, True)
             res = keep.tile([P, 2, P], F32, name=f"res{vb}")

@@ -180,7 +180,6 @@ def tile_picked_ymeshcnn_lin_p_kernel(
         nc.vector.tensor_copy(woven(w65_bf[:, W : 2 * W]), planes(w5_raw[:]))
         nc.vector.tensor_copy(woven(w2_bf[:]), planes(w2_raw[:]))
         w65_q = quantize(w65_bf[:], "w65")
-        w2_q = quantize(w2_bf[:], "w2")
 
         hb, hd = f32_tile("hb", "w1_codes"), f32_tile("hd")
         for t in range(PACK):
@@ -202,16 +201,15 @@ def tile_picked_ymeshcnn_lin_p_kernel(
         ds1_bf = bf_tile("ds1_bf", 2 * W, "w2_raw")
         total(ds1_bf[:, W : 2 * W], ha, hc)
         copy_back(ds1_bf[:, 0:W], banks[3])
+        w2_q = quantize(w2_bf[:], "w2")
         ds1_q = quantize(ds1_bf[:], "ds1")
         product(w43_q, 0, ds1_q, 0, True)
         product(w43_q, N, ds1_q, V, False)
         s2_bf = bf_tile("s2_bf", W, "ha")
         d2_bf = bf_tile("d2_bf", W, "w2_raw")
         total(s2_bf[:], hb, hd)
-        s2_q = quantize(s2_bf[:], "s2")
         copy_back(d2_bf[:], banks[4])
-        product(w65_q, N, s2_q, 0, False)
-        product(w65_q, 0, quantize(d2_bf[:], "d2"), 0, False)
+        product(w65_q, N, quantize(s2_bf[:], "s2"), 0, False)
         hown = keep.tile([P, 2 * PACK * P], F32, name="hown", align_bytes=64)
         for vb in range(2):
             half = hown[:, PACK * P * vb : PACK * P * (vb + 1)].rearrange("p (t v) -> p t v", t=PACK)
@@ -219,6 +217,8 @@ def tile_picked_ymeshcnn_lin_p_kernel(
                 gather(half[:, t, :], t, own_t[:, 8 * vb : 8 * (vb + 1)], False)
             own_bf = bf_tile(f"own_bf{vb}", PACK * P, ("hd", "w1_codes")[vb])
             nc.vector.tensor_copy(woven(own_bf[:]), planes(half))
+            if vb == 0:
+                product(w65_q, 0, quantize(d2_bf[:], "d2"), 0, False)
             half_product(w2_q, 0, quantize(own_bf[:], f"own{vb}"), 0, vb, False, True)
             res = keep.tile([P, 2, P], F32, name=f"res{vb}")
             nc.scalar.activation(res[:, 0, :], out_acc[vb][0], ACT.Copy)

@@ -91,23 +91,11 @@ def tile_picked_ymeshcnn_lin_p_kernel(
         x_codes = [keep.tile([P, S // 2], U32, name=f"x_codes{u}", align_bytes=64) for u in range(2)]
         for u in range(2):
             nc.vector.tensor_copy(x_codes[u][:], xw_all[:].indirect(offs_t[:, 16 * u : 16 * (u + 1)]))
-        h = [keep.tile([P, S], F32, name=f"h{t}", align_bytes=64) for t in range(PACK)]
 
         def first_layer(acc, t, u):
             nc.tensor.matmul_mx(
                 out=acc, lhsT=w1_q[0][:, P * t : P * (t + 1)].bitcast(FP8X4), lhsT_scale=w1_q[1][:, P * t : P * (t + 1)],
                 rhs=x_codes[u][:].bitcast(FP8X4), rhs_scale=x_scale[:, halves[u]], start=True, stop=True)
-
-        for u in range(2):
-            for t in range(2):
-                acc = banks[(0, 2, 1, 7)[2 * u + t]][:, 0 : S // 2]
-                first_layer(acc, t, u)
-                nc.scalar.activation(h[t][:, halves[u]], acc, ACT.Copy)
-        for t in range(2, PACK):
-            for u in range(2):
-                first_layer(banks[1 + t][:, halves[u]], t, u)
-        nc.scalar.activation(h[2][:], banks[3][:], ACT.Copy)
-        nc.vector.tensor_copy(h[3][:], banks[4][:])
 
         def woven(dst):
             return dst.rearrange("p (c i t) -> p c t i", i=LINE, t=PACK)
@@ -120,6 +108,21 @@ def tile_picked_ymeshcnn_lin_p_kernel(
 
         def f32_tile(name, slot=None):
             return keep.tile([P, PACK, V], F32, name=name, tag=slot or name, align_bytes=64)
+
+        W = N * PACK
+        w4_bf = bf_tile("w4_bf", W)
+        nc.vector.tensor_copy(woven(w4_bf[:]), planes(w4_raw[:]))
+        h = [keep.tile([P, S], F32, name=f"h{t}", align_bytes=64) for t in range(PACK)]
+        for u in range(2):
+            for t in range(2):
+                acc = banks[(0, 2, 1, 7)[2 * u + t]][:, 0 : S // 2]
+                first_layer(acc, t, u)
+                nc.scalar.activation(h[t][:, halves[u]], acc, ACT.Copy)
+        w4_q = quantize(w4_bf[:], "w4")
+        for t in range(2, PACK):
+            for u in range(2):
+                first_layer(banks[1 + t][:, halves[u]], t, u)
+            nc.scalar.activation(h[t][:], banks[1 + t][:], ACT.Copy)
 
         def gather(dst, t, places, on_vector):
             if on_vector:
@@ -159,8 +162,7 @@ def tile_picked_ymeshcnn_lin_p_kernel(
             nc.vector.tensor_copy(dst.bitcast(F32).rearrange("p (b v u) -> p b v u", b=2, u=2),
                                   back[:].rearrange("p (b u v) -> p b v u", b=2, u=2))
 
-        W = N * PACK
-        ha, hc = f32_tile("ha"), f32_tile("hc")
+        ha, hc = f32_tile("ha", "w4_bf"), f32_tile("hc")
         acc1, acc2 = banks[0:2], banks[5:7]
         for t in range(PACK):
             gather(ha[:, t, :], t, ea_t[:], True)
@@ -170,24 +172,17 @@ def tile_picked_ymeshcnn_lin_p_kernel(
         turn_back(acc1, "rows1", banks[3], 0)
         turn_back(acc1, "rows1", banks[3], 1)
 
-        w43_bf = bf_tile("w43_bf", 2 * W)
-        w65_bf = bf_tile("w65_bf", 2 * W)
-        w2_bf = bf_tile("w2_bf", W)
-        nc.vector.tensor_copy(woven(w43_bf[:, 0:W]), planes(w4_raw[:]))
-        nc.vector.tensor_copy(woven(w43_bf[:, W : 2 * W]), planes(w3_raw[:]))
-        nc.vector.tensor_copy(woven(w65_bf[:, 0:W]), planes(w6_raw[:]))
-        w43_q = quantize(w43_bf[:], "w43")
-        nc.vector.tensor_copy(woven(w65_bf[:, W : 2 * W]), planes(w5_raw[:]))
-        nc.vector.tensor_copy(woven(w2_bf[:]), planes(w2_raw[:]))
-        w65_q = quantize(w65_bf[:], "w65")
+        w36_bf = bf_tile("w36_bf", 2 * W)
+        w52_bf = bf_tile("w52_bf", 2 * W)
+        nc.vector.tensor_copy(woven(w36_bf[:, 0:W]), planes(w3_raw[:]))
+        nc.vector.tensor_copy(woven(w36_bf[:, W : 2 * W]), planes(w6_raw[:]))
+        nc.vector.tensor_copy(woven(w52_bf[:, 0:W]), planes(w5_raw[:]))
+        w36_q = quantize(w36_bf[:], "w36")
+        nc.vector.tensor_copy(woven(w52_bf[:, W : 2 * W]), planes(w2_raw[:]))
 
         hb, hd = f32_tile("hb", "w1_codes"), f32_tile("hd")
         for t in range(PACK):
-            if t == 0:
-                gather(hb[:, t, 0:P], t, eb_t[:, 0:8], True)
-                gather(hb[:, t, P:V], t, eb_t[:, 8:16], False)
-            else:
-                gather(hb[:, t, :], t, eb_t[:], False)
+            gather(hb[:, t, :], t, eb_t[:], t < 2)
             add_transposed(hb, t, acc2, True)
         for t in range(PACK):
             gather_negated(hd[:, t, :], t, ed_t[:])
@@ -201,15 +196,15 @@ def tile_picked_ymeshcnn_lin_p_kernel(
         ds1_bf = bf_tile("ds1_bf", 2 * W, "w2_raw")
         total(ds1_bf[:, W : 2 * W], ha, hc)
         copy_back(ds1_bf[:, 0:W], banks[3])
-        w2_q = quantize(w2_bf[:], "w2")
+        w52_q = quantize(w52_bf[:], "w52")
         ds1_q = quantize(ds1_bf[:], "ds1")
-        product(w43_q, 0, ds1_q, 0, True)
-        product(w43_q, N, ds1_q, V, False)
-        s2_bf = bf_tile("s2_bf", W, "ha")
+        product(w4_q, 0, ds1_q, 0, True)
+        product(w36_q, 0, ds1_q, V, False)
+        s2_bf = bf_tile("s2_bf", W, "w4_bf")
         d2_bf = bf_tile("d2_bf", W, "w2_raw")
         total(s2_bf[:], hb, hd)
         copy_back(d2_bf[:], banks[4])
-        product(w65_q, N, quantize(s2_bf[:], "s2"), 0, False)
+        product(w52_q, 0, quantize(s2_bf[:], "s2"), 0, False)
         hown = keep.tile([P, 2 * PACK * P], F32, name="hown", align_bytes=64)
         for vb in range(2):
             half = hown[:, PACK * P * vb : PACK * P * (vb + 1)].rearrange("p (t v) -> p t v", t=PACK)
@@ -218,8 +213,8 @@ def tile_picked_ymeshcnn_lin_p_kernel(
             own_bf = bf_tile(f"own_bf{vb}", PACK * P, ("hd", "w1_codes")[vb])
             nc.vector.tensor_copy(woven(own_bf[:]), planes(half))
             if vb == 0:
-                product(w65_q, 0, quantize(d2_bf[:], "d2"), 0, False)
-            half_product(w2_q, 0, quantize(own_bf[:], f"own{vb}"), 0, vb, False, True)
+                product(w36_q, N, quantize(d2_bf[:], "d2"), 0, False)
+            half_product(w52_q, N, quantize(own_bf[:], f"own{vb}"), 0, vb, False, True)
             res = keep.tile([P, 2, P], F32, name=f"res{vb}")
             nc.scalar.activation(res[:, 0, :], out_acc[vb][0], ACT.Copy)
             if vb == 0:

@@ -48,10 +48,10 @@ def tile_picked_ymeshcnn_lin_p_kernel(
             nc.sync.dma_start(xs_all[32 * q : 32 * q + 4, :].bitcast(I32), x_scales[0, 4 * q : 4 * q + 4, :].bitcast(I32))
         xw_all = keep.tile([P, T], U32, name="xw_all")
         nc.sync.dma_start(xw_all[:].bitcast(I32), x_words[0].rearrange("p n t -> p (n t)").bitcast(I32))
-        ea_t = load_list(ea, "ea_t")
         ec_t = load_list(ec, "ec_t")
         w4_raw = load_weight(w4, "w4_raw")
         w3_raw = load_weight(w3, "w3_raw")
+        ea_t = load_list(ea, "ea_t")
         eb_t = load_list(eb, "eb_t")
         w6_raw = load_weight(w6, "w6_raw")
         ed_t = load_list(ed, "ed_t")
@@ -113,16 +113,6 @@ def tile_picked_ymeshcnn_lin_p_kernel(
         w4_bf = bf_tile("w4_bf", W)
         nc.vector.tensor_copy(woven(w4_bf[:]), planes(w4_raw[:]))
         h = [keep.tile([P, S], F32, name=f"h{t}", align_bytes=64) for t in range(PACK)]
-        for u in range(2):
-            for t in range(2):
-                acc = banks[(0, 2, 1, 7)[2 * u + t]][:, 0 : S // 2]
-                first_layer(acc, t, u)
-                nc.scalar.activation(h[t][:, halves[u]], acc, ACT.Copy)
-        w4_q = quantize(w4_bf[:], "w4")
-        for t in range(2, PACK):
-            for u in range(2):
-                first_layer(banks[1 + t][:, halves[u]], t, u)
-            nc.scalar.activation(h[t][:], banks[1 + t][:], ACT.Copy)
 
         def gather(dst, t, places, on_vector):
             if on_vector:
@@ -132,6 +122,19 @@ def tile_picked_ymeshcnn_lin_p_kernel(
 
         def gather_negated(dst, t, places):
             nc.scalar.activation(dst, h[t][:].indirect(places), ACT.Copy, scale=-1.0)
+
+        for u in range(2):
+            for t in range(2):
+                acc = banks[(0, 2, 1, 7)[2 * u + t]][:, 0 : S // 2]
+                first_layer(acc, t, u)
+                nc.scalar.activation(h[t][:, halves[u]], acc, ACT.Copy)
+        w4_q = quantize(w4_bf[:], "w4")
+        hc = f32_tile("hc")
+        gather_negated(hc[:, 0, :], 0, ec_t[:])
+        for t in range(2, PACK):
+            for u in range(2):
+                first_layer(banks[1 + t][:, halves[u]], t, u)
+            nc.scalar.activation(h[t][:], banks[1 + t][:], ACT.Copy)
 
         out_acc = [[banks[5][:, 0:P], banks[6][:, 0:P]], [banks[0][:, 0:P], banks[1][:, 0:P]]]
 
@@ -162,19 +165,20 @@ def tile_picked_ymeshcnn_lin_p_kernel(
             nc.vector.tensor_copy(dst.bitcast(F32).rearrange("p (b v u) -> p b v u", b=2, u=2),
                                   back[:].rearrange("p (b u v) -> p b v u", b=2, u=2))
 
-        ha, hc = f32_tile("ha", "w4_bf"), f32_tile("hc")
+        w36_bf = bf_tile("w36_bf", 2 * W)
+        nc.vector.tensor_copy(woven(w36_bf[:, 0:W]), planes(w3_raw[:]))
+        ha = f32_tile("ha", "w3_raw")
         acc1, acc2 = banks[0:2], banks[5:7]
         for t in range(PACK):
             gather(ha[:, t, :], t, ea_t[:], True)
-            gather_negated(hc[:, t, :], t, ec_t[:])
+            if t > 0:
+                gather_negated(hc[:, t, :], t, ec_t[:])
             add_transposed(ha, t, acc1, True)
             add_transposed(hc, t, acc1, False)
         turn_back(acc1, "rows1", banks[3], 0)
         turn_back(acc1, "rows1", banks[3], 1)
 
-        w36_bf = bf_tile("w36_bf", 2 * W)
         w52_bf = bf_tile("w52_bf", 2 * W)
-        nc.vector.tensor_copy(woven(w36_bf[:, 0:W]), planes(w3_raw[:]))
         nc.vector.tensor_copy(woven(w36_bf[:, W : 2 * W]), planes(w6_raw[:]))
         nc.vector.tensor_copy(woven(w52_bf[:, 0:W]), planes(w5_raw[:]))
         w36_q = quantize(w36_bf[:], "w36")
@@ -200,7 +204,7 @@ def tile_picked_ymeshcnn_lin_p_kernel(
         ds1_q = quantize(ds1_bf[:], "ds1")
         product(w4_q, 0, ds1_q, 0, True)
         product(w36_q, 0, ds1_q, V, False)
-        s2_bf = bf_tile("s2_bf", W, "w4_bf")
+        s2_bf = bf_tile("s2_bf", W, "w3_raw")
         d2_bf = bf_tile("d2_bf", W, "w2_raw")
         total(s2_bf[:], hb, hd)
         copy_back(d2_bf[:], banks[4])

@@ -19,7 +19,7 @@ ACT = mybir.ActivationFunctionType
 P = 128
 PACK = 4
 LINE = 2
-W1_SCALAR_M = 64
+W1_SCALAR_M = 80
 
 
 def tile_picked_ymeshcnn_lin_p_kernel(
@@ -52,11 +52,11 @@ def tile_picked_ymeshcnn_lin_p_kernel(
         w4_raw = load_weight(w4, "w4_raw")
         w3_raw = load_weight(w3, "w3_raw")
         ea_t = load_list(ea, "ea_t")
-        eb_t = load_list(eb, "eb_t")
         w6_raw = load_weight(w6, "w6_raw")
-        ed_t = load_list(ed, "ed_t")
+        eb_t = load_list(eb, "eb_t")
         w5_raw = load_weight(w5, "w5_raw")
         w2_raw = load_weight(w2, "w2_raw")
+        ed_t = load_list(ed, "ed_t")
         own_t = load_list(own, "own_t")
 
         w1_bf = keep.tile([P, PACK, P, PACK], BF16, name="w1_bf", align_bytes=64)
@@ -165,9 +165,7 @@ def tile_picked_ymeshcnn_lin_p_kernel(
             nc.vector.tensor_copy(dst.bitcast(F32).rearrange("p (b v u) -> p b v u", b=2, u=2),
                                   back[:].rearrange("p (b u v) -> p b v u", b=2, u=2))
 
-        w36_bf = bf_tile("w36_bf", 2 * W)
-        nc.vector.tensor_copy(woven(w36_bf[:, 0:W]), planes(w3_raw[:]))
-        ha = f32_tile("ha", "w3_raw")
+        ha = f32_tile("ha", "w4_raw")
         acc1, acc2 = banks[0:2], banks[5:7]
         for t in range(PACK):
             gather(ha[:, t, :], t, ea_t[:], True)
@@ -178,7 +176,9 @@ def tile_picked_ymeshcnn_lin_p_kernel(
         turn_back(acc1, "rows1", banks[3], 0)
         turn_back(acc1, "rows1", banks[3], 1)
 
+        w36_bf = bf_tile("w36_bf", 2 * W)
         w52_bf = bf_tile("w52_bf", 2 * W)
+        nc.vector.tensor_copy(woven(w36_bf[:, 0:W]), planes(w3_raw[:]))
         nc.vector.tensor_copy(woven(w36_bf[:, W : 2 * W]), planes(w6_raw[:]))
         nc.vector.tensor_copy(woven(w52_bf[:, 0:W]), planes(w5_raw[:]))
         w36_q = quantize(w36_bf[:], "w36")
@@ -186,10 +186,14 @@ def tile_picked_ymeshcnn_lin_p_kernel(
 
         hb, hd = f32_tile("hb", "w1_codes"), f32_tile("hd")
         for t in range(PACK):
-            gather(hb[:, t, :], t, eb_t[:], t < 2)
+            if t == 2:
+                gather(hb[:, t, 0:P], t, eb_t[:, 0:8], True)
+                gather(hb[:, t, P:V], t, eb_t[:, 8:16], False)
+            else:
+                gather(hb[:, t, :], t, (ed_t if t == 1 else eb_t)[:], t < 2)
             add_transposed(hb, t, acc2, True)
         for t in range(PACK):
-            gather_negated(hd[:, t, :], t, ed_t[:])
+            gather_negated(hd[:, t, :], t, (eb_t if t == 1 else ed_t)[:])
             add_transposed(hd, t, acc2, False)
         turn_back(acc2, "rows2", banks[4], 0)
         turn_back(acc2, "rows2", banks[4], 1)
@@ -204,12 +208,12 @@ def tile_picked_ymeshcnn_lin_p_kernel(
         ds1_q = quantize(ds1_bf[:], "ds1")
         product(w4_q, 0, ds1_q, 0, True)
         product(w36_q, 0, ds1_q, V, False)
-        s2_bf = bf_tile("s2_bf", W, "w3_raw")
+        s2_bf = bf_tile("s2_bf", W, "w4_raw")
         d2_bf = bf_tile("d2_bf", W, "w2_raw")
         total(s2_bf[:], hb, hd)
         copy_back(d2_bf[:], banks[4])
         product(w52_q, 0, quantize(s2_bf[:], "s2"), 0, False)
-        hown = keep.tile([P, 2 * PACK * P], F32, name="hown", align_bytes=64)
+        hown = keep.tile([P, 2 * PACK * P], F32, name="hown", tag="hc", align_bytes=64)
         for vb in range(2):
             half = hown[:, PACK * P * vb : PACK * P * (vb + 1)].rearrange("p (t v) -> p t v", t=PACK)
             for t in range(PACK):

@@ -19,7 +19,7 @@ ACT = mybir.ActivationFunctionType
 P = 128
 PACK = 4
 LINE = 2
-W1_SCALAR_M = 80
+W1_SCALAR_M = 64
 
 
 def tile_picked_ymeshcnn_lin_p_kernel(
@@ -41,11 +41,14 @@ def tile_picked_ymeshcnn_lin_p_kernel(
             return tile
 
         xs_all = keep.tile([P, T], U8, name="xs_all")
-        nc.vector.memset(xs_all[:].bitcast(I32), 0)
+        nc.gpsimd.memset(xs_all[:].bitcast(I32), 0)
         offs_t = load_list(offs, "offs_t")
-        w1_raw = load_weight(w1, "w1_raw")
+        w1_raw = keep.tile([P, PACK, H], F32, name="w1_raw", align_bytes=64)
+        w1_rows = w1.rearrange("(p j) n -> p j n", j=PACK)
+        nc.sync.dma_start(w1_raw[:, 0:2, :], w1_rows[:, 0:2, :])
         for q in range(4):
             nc.sync.dma_start(xs_all[32 * q : 32 * q + 4, :].bitcast(I32), x_scales[0, 4 * q : 4 * q + 4, :].bitcast(I32))
+        nc.sync.dma_start(w1_raw[:, 2:4, :], w1_rows[:, 2:4, :])
         xw_all = keep.tile([P, T], U32, name="xw_all")
         nc.sync.dma_start(xw_all[:].bitcast(I32), x_words[0].rearrange("p n t -> p (n t)").bitcast(I32))
         ec_t = load_list(ec, "ec_t")
@@ -61,13 +64,14 @@ def tile_picked_ymeshcnn_lin_p_kernel(
 
         w1_bf = keep.tile([P, PACK, P, PACK], BF16, name="w1_bf", align_bytes=64)
 
-        def w1_views(m0, m1):
-            dst = w1_bf[:, :, m0:m1, :].rearrange("p t m j -> p m j t")
-            src = w1_raw[:, :, PACK * m0 : PACK * m1].rearrange("p j (m t) -> p m j t", t=PACK)
+        def w1_views(m0, m1, j0, j1):
+            dst = w1_bf[:, :, m0:m1, j0:j1].rearrange("p t m j -> p m j t")
+            src = w1_raw[:, j0:j1, PACK * m0 : PACK * m1].rearrange("p j (m t) -> p m j t", t=PACK)
             return dst, src
 
-        nc.scalar.activation(*w1_views(0, W1_SCALAR_M), ACT.Copy)
-        nc.vector.tensor_copy(*w1_views(W1_SCALAR_M, P))
+        nc.scalar.activation(*w1_views(0, W1_SCALAR_M, 0, 2), ACT.Copy)
+        nc.scalar.activation(*w1_views(0, W1_SCALAR_M, 2, 4), ACT.Copy)
+        nc.vector.tensor_copy(*w1_views(W1_SCALAR_M, P, 0, 4))
 
         def quantize(src, name, slot=None):
             width = src.shape[1] // PACK

from contextlib import ExitStack

import concourse.mybir as mybir
from concourse.masks import make_identity

K, T, S, H, N, V = 512, 2048, 512, 512, 256, 256
FLOPS = 2 * K * H * S + 5 * 2 * H * N * V

F32 = mybir.dt.float32
BF16 = mybir.dt.bfloat16
I32 = mybir.dt.int32
U32 = mybir.dt.uint32
U16 = mybir.dt.uint16
U8 = mybir.dt.uint8
FP8X4 = mybir.dt.float8_e4m3fn_x4
ALU = mybir.AluOpType
ACT = mybir.ActivationFunctionType

P = 128
PACK = 4
LINE = 2
W1_SCALAR_M = 64


def tile_picked_ymeshcnn_lin_p_kernel(
    tc, x_words, x_scales, w1, w2, w3, w4, w5, w6, offs, own, ea, eb, ec, ed, out
):
    nc = tc.nc
    with ExitStack() as ctx:
        keep = ctx.enter_context(tc.tile_pool(name="keep", bufs=1))
        psum = ctx.enter_context(tc.psum_pool(name="psum", bufs=1))

        def load_list(src, name):
            tile = keep.tile(list(src.shape), U16, name=name)
            nc.sync.dma_start(tile[:], src)
            return tile

        def load_weight(src, name):
            tile = keep.tile([P, PACK, src.shape[1]], F32, name=name, align_bytes=64)
            nc.sync.dma_start(tile[:], src.rearrange("(p j) n -> p j n", j=PACK))
            return tile

        xs_all = keep.tile([P, T], U8, name="xs_all")
        nc.gpsimd.memset(xs_all[:].bitcast(I32), 0)
        offs_t = load_list(offs, "offs_t")
        w1_raw = keep.tile([P, PACK, H], F32, name="w1_raw", align_bytes=64)
        w1_rows = w1.rearrange("(p j) n -> p j n", j=PACK)
        nc.sync.dma_start(w1_raw[:, 0:2, :], w1_rows[:, 0:2, :])
        for q in range(4):
            nc.sync.dma_start(xs_all[32 * q : 32 * q + 4, :].bitcast(I32), x_scales[0, 4 * q : 4 * q + 4, :].bitcast(I32))
        nc.sync.dma_start(w1_raw[:, 2:4, :], w1_rows[:, 2:4, :])
        xw_all = keep.tile([P, T], U32, name="xw_all")
        nc.sync.dma_start(xw_all[:].bitcast(I32), x_words[0].rearrange("p n t -> p (n t)").bitcast(I32))
        ec_t = load_list(ec, "ec_t")
        w4_raw = load_weight(w4, "w4_raw")
        w3_raw = load_weight(w3, "w3_raw")
        ea_t = load_list(ea, "ea_t")
        w6_raw = load_weight(w6, "w6_raw")
        eb_t = load_list(eb, "eb_t")
        w5_raw = load_weight(w5, "w5_raw")
        w2_raw = load_weight(w2, "w2_raw")
        ed_t = load_list(ed, "ed_t")
        own_t = load_list(own, "own_t")

        w1_bf = keep.tile([P, PACK, P, PACK], BF16, name="w1_bf", align_bytes=64)

        def w1_views(m0, m1, j0, j1):
            dst = w1_bf[:, :, m0:m1, j0:j1].rearrange("p t m j -> p m j t")
            src = w1_raw[:, j0:j1, PACK * m0 : PACK * m1].rearrange("p j (m t) -> p m j t", t=PACK)
            return dst, src

        nc.scalar.activation(*w1_views(0, W1_SCALAR_M, 0, 2), ACT.Copy)
        nc.scalar.activation(*w1_views(0, W1_SCALAR_M, 2, 4), ACT.Copy)
        nc.vector.tensor_copy(*w1_views(W1_SCALAR_M, P, 0, 4))

        def quantize(src, name, slot=None):
            width = src.shape[1] // PACK
            codes = keep.tile([P, width], U32, name=name + "_codes", tag=slot or name + "_codes", align_bytes=64)
            scale = keep.tile([P, width], U8, name=name + "_scale", align_bytes=64)
            nc.vector.quantize_mx(out=codes[:].bitcast(FP8X4), scales=scale[:], in_=src)
            return codes, scale

        def mx(acc, lhs, lcols, rhs, rcols, start, stop):
            nc.tensor.matmul_mx(
                out=acc, lhsT=lhs[0][:, lcols].bitcast(FP8X4), lhsT_scale=lhs[1][:, lcols],
                rhs=rhs[0][:, rcols].bitcast(FP8X4), rhs_scale=rhs[1][:, rcols], start=start, stop=stop)

        banks = [psum.tile([P, 512], F32, name=f"bank{b}") for b in range(8)]
        ident = keep.tile([P, P], F32, name="ident")
        make_identity(nc, ident[:])
        x_scale = keep.tile([P, S], U8, name="x_scale", align_bytes=64)
        nc.vector.tensor_copy(x_scale[:], xs_all[:].indirect(offs_t[:]))
        w1_q = quantize(w1_bf[:].rearrange("p t m j -> p (t m j)"), "w1")
        halves = [slice(0, S // 2), slice(S // 2, S)]
        x_codes = [keep.tile([P, S // 2], U32, name=f"x_codes{u}", align_bytes=64) for u in range(2)]
        for u in range(2):
            nc.vector.tensor_copy(x_codes[u][:], xw_all[:].indirect(offs_t[:, 16 * u : 16 * (u + 1)]))

        def first_layer(acc, t, u):
            nc.tensor.matmul_mx(
                out=acc, lhsT=w1_q[0][:, P * t : P * (t + 1)].bitcast(FP8X4), lhsT_scale=w1_q[1][:, P * t : P * (t + 1)],
                rhs=x_codes[u][:].bitcast(FP8X4), rhs_scale=x_scale[:, halves[u]], start=True, stop=True)

        def woven(dst):
            return dst.rearrange("p (c i t) -> p c t i", i=LINE, t=PACK)

        def planes(src):
            return src.rearrange("p t (c i) -> p c t i", i=LINE)

        def bf_tile(name, width, slot=None):
            return keep.tile([P, width], BF16, name=name, tag=slot or name, align_bytes=64)

        def f32_tile(name, slot=None):
            return keep.tile([P, PACK, V], F32, name=name, tag=slot or name, align_bytes=64)

        W = N * PACK
        w4_bf = bf_tile("w4_bf", W)
        nc.vector.tensor_copy(woven(w4_bf[:]), planes(w4_raw[:]))
        h = [keep.tile([P, S], F32, name=f"h{t}", align_bytes=64) for t in range(PACK)]

        def gather(dst, t, places, on_vector):
            if on_vector:
                nc.vector.tensor_copy(dst, h[t][:].indirect(places))
            else:
                nc.scalar.activation(dst, h[t][:].indirect(places), ACT.Copy)

        def gather_negated(dst, t, places):
            nc.scalar.activation(dst, h[t][:].indirect(places), ACT.Copy, scale=-1.0)

        for u in range(2):
            for t in range(2):
                acc = banks[(0, 2, 1, 7)[2 * u + t]][:, 0 : S // 2]
                first_layer(acc, t, u)
                nc.scalar.activation(h[t][:, halves[u]], acc, ACT.Copy)
        w4_q = quantize(w4_bf[:], "w4")
        hc = f32_tile("hc")
        gather_negated(hc[:, 0, :], 0, ec_t[:])
        for t in range(2, PACK):
            for u in range(2):
                first_layer(banks[1 + t][:, halves[u]], t, u)
            nc.scalar.activation(h[t][:], banks[1 + t][:], ACT.Copy)

        out_acc = [[banks[5][:, 0:P], banks[6][:, 0:P]], [banks[0][:, 0:P], banks[1][:, 0:P]]]

        def half_product(w_q, w0, v_q, v0, vb, start, stop):
            for m in range(2):
                mx(out_acc[vb][m], w_q, slice(w0 + P * m, w0 + P * (m + 1)), v_q, slice(v0, v0 + P), start, stop)

        def product(w_q, w0, v_q, v0, start):
            for vb in range(2):
                half_product(w_q, w0, v_q, v0 + P * vb, vb, start, False)

        def add_transposed(src, t, acc, first):
            for vb in range(2):
                at = P * (2 * vb + t % 2)
                nc.tensor.matmul(acc[t // 2][:, at : at + P], src[:, t, P * vb : P * (vb + 1)], ident[:],
                                 start=(first and t % 2 == 0 and vb == 0),
                                 stop=(not first and t % 2 == 1 and vb == 1), is_transpose=True)

        def turn_back(acc, name, back, u):
            half = bf_tile(f"{name}_{u}", 512)[:]
            nc.scalar.activation(half.rearrange("v (b p e) -> v b p e", b=2, e=2),
                                 acc[u][:].rearrange("v (b e p) -> v b p e", b=2, e=2), ACT.Abs)
            words = half.bitcast(F32)
            for vb in range(2):
                nc.tensor.transpose(back[:, P * (2 * vb + u) : P * (2 * vb + u + 1)], words[:, P * vb : P * (vb + 1)], ident[:])

        def copy_back(dst, back):
            nc.vector.tensor_copy(dst.bitcast(F32).rearrange("p (b v u) -> p b v u", b=2, u=2),
                                  back[:].rearrange("p (b u v) -> p b v u", b=2, u=2))

        ha = f32_tile("ha", "w4_raw")
        acc1, acc2 = banks[0:2], banks[5:7]
        for t in range(PACK):
            gather(ha[:, t, :], t, ea_t[:], True)
            if t > 0:
                gather_negated(hc[:, t, :], t, ec_t[:])
            add_transposed(ha, t, acc1, True)
            add_transposed(hc, t, acc1, False)
        turn_back(acc1, "rows1", banks[3], 0)
        turn_back(acc1, "rows1", banks[3], 1)

        w36_bf = bf_tile("w36_bf", 2 * W)
        w52_bf = bf_tile("w52_bf", 2 * W)
        nc.vector.tensor_copy(woven(w36_bf[:, 0:W]), planes(w3_raw[:]))
        nc.vector.tensor_copy(woven(w36_bf[:, W : 2 * W]), planes(w6_raw[:]))
        nc.vector.tensor_copy(woven(w52_bf[:, 0:W]), planes(w5_raw[:]))
        w36_q = quantize(w36_bf[:], "w36")
        nc.vector.tensor_copy(woven(w52_bf[:, W : 2 * W]), planes(w2_raw[:]))

        hb, hd = f32_tile("hb", "w1_codes"), f32_tile("hd")
        for t in range(PACK):
            if t == 2:
                gather(hb[:, t, 0:P], t, eb_t[:, 0:8], True)
                gather(hb[:, t, P:V], t, eb_t[:, 8:16], False)
            else:
                gather(hb[:, t, :], t, (ed_t if t == 1 else eb_t)[:], t < 2)
            add_transposed(hb, t, acc2, True)
        for t in range(PACK):
            gather_negated(hd[:, t, :], t, (eb_t if t == 1 else ed_t)[:])
            add_transposed(hd, t, acc2, False)
        turn_back(acc2, "rows2", banks[4], 0)
        turn_back(acc2, "rows2", banks[4], 1)

        def total(dst, first, negated):
            nc.vector.tensor_tensor(woven(dst), planes(first[:]), planes(negated[:]), ALU.subtract)

        ds1_bf = bf_tile("ds1_bf", 2 * W, "w2_raw")
        total(ds1_bf[:, W : 2 * W], ha, hc)
        copy_back(ds1_bf[:, 0:W], banks[3])
        w52_q = quantize(w52_bf[:], "w52")
        ds1_q = quantize(ds1_bf[:], "ds1")
        product(w4_q, 0, ds1_q, 0, True)
        product(w36_q, 0, ds1_q, V, False)
        s2_bf = bf_tile("s2_bf", W, "w4_raw")
        d2_bf = bf_tile("d2_bf", W, "w2_raw")
        total(s2_bf[:], hb, hd)
        copy_back(d2_bf[:], banks[4])
        product(w52_q, 0, quantize(s2_bf[:], "s2"), 0, False)
        hown = keep.tile([P, 2 * PACK * P], F32, name="hown", tag="hc", align_bytes=64)
        for vb in range(2):
            half = hown[:, PACK * P * vb : PACK * P * (vb + 1)].rearrange("p (t v) -> p t v", t=PACK)
            for t in range(PACK):
                gather(half[:, t, :], t, own_t[:, 8 * vb : 8 * (vb + 1)], False)
            own_bf = bf_tile(f"own_bf{vb}", PACK * P, ("hd", "w1_codes")[vb])
            nc.vector.tensor_copy(woven(own_bf[:]), planes(half))
            if vb == 0:
                product(w36_q, N, quantize(d2_bf[:], "d2"), 0, False)
            half_product(w52_q, N, quantize(own_bf[:], f"own{vb}"), 0, vb, False, True)
            res = keep.tile([P, 2, P], F32, name=f"res{vb}")
            nc.scalar.activation(res[:, 0, :], out_acc[vb][0], ACT.Copy)
            if vb == 0:
                nc.scalar.activation(res[:, 1, :], out_acc[vb][1], ACT.Copy)
            else:
                nc.vector.tensor_copy(res[:, 1, :], out_acc[vb][1])
            nc.sync.dma_start(out[:, P * vb : P * (vb + 1)].rearrange("(m p) v -> p m v", m=2), res[:])
